import numpy as np
import ml_dtypes


def mxq(x, axis, fmt="e4m3"):
    dtype, down = {"e4m3": (ml_dtypes.float8_e4m3fn, 7), "e5m2": (ml_dtypes.float8_e5m2, 14)}[fmt]
    v = np.moveaxis(np.asarray(x, np.float32).astype(ml_dtypes.bfloat16).astype(np.float64), axis, -1)
    blocks = v.reshape(v.shape[:-1] + (-1, 32))
    amax = np.abs(blocks).max(-1, keepdims=True)
    byte = np.maximum(np.where(amax > 0, np.frexp(amax)[1] - 1 + 127, 0) - down, 1)
    scale = np.exp2(byte - 127.0)
    codes = (blocks / scale).astype(np.float32).astype(dtype).astype(np.float64)
    return np.moveaxis((codes * scale).reshape(v.shape), -1, axis)


WIDE = False


def mx_kscale(k):
    if not WIDE:
        return np.ones(k)
    levels = np.array([10, -10, 5, -5, 0])
    if k % 512:
        return np.exp2(np.random.permutation(np.resize(levels, k // 32))).repeat(32)
    a = np.empty((k // 512, 16))
    for p in range(k // 512):
        a[p, :8] = np.random.permutation(np.resize(levels, 8))
        for g in range(8):
            far = levels[np.abs(levels - a[p, g]) >= 10]
            a[p, g + 8] = far[np.random.randint(len(far))]
    return np.exp2(a.ravel()).repeat(32)


def f64(x):
    return np.asarray(x).astype(np.float64)


def striped(idx):
    return np.tile(idx.reshape(-1, 16).T, (8, 1)).astype(np.uint16)


def unstriped(offs):
    return offs[:16].T.reshape(-1).astype(np.int64)


E2M1 = np.array([0.0, 0.5, 1.0, 1.5, 2.0, 3.0, 4.0, 6.0, -0.0, -0.5, -1.0, -1.5, -2.0, -3.0, -4.0, -6.0])


def pack_weight(w, fmt):
    k, n = w.shape
    w = f64(np.asarray(w, np.float32).astype(ml_dtypes.bfloat16)).reshape(k // 32, 32, n)
    amax = np.abs(w).max(1)
    if fmt == "e4m3":
        byte = np.frexp(amax)[1] - 1 + 127 - 7
    else:
        mant, ex = np.frexp(amax / 6.0)
        byte = np.where(mant > 0.5, ex, ex - 1) + 127
    byte = np.clip(np.where(amax > 0, byte, 1), 1, 254)
    scaled = (w * np.exp2(127.0 - byte)[:, None, :]).reshape(k, n).astype(np.float32)
    by_word = np.ascontiguousarray(scaled.reshape(k // 512, 128, 4, n).transpose(0, 1, 3, 2))
    if fmt == "e4m3":
        words = by_word.astype(ml_dtypes.float8_e4m3fn).view(np.uint8)
    else:
        c = by_word.astype(ml_dtypes.float4_e2m1fn).view(np.uint8) & 0xF
        words = (c[..., 0::2] | (c[..., 1::2] << 4)).reshape(k // 512, 128, 2 * n)
    return np.ascontiguousarray(words), np.ascontiguousarray(byte.astype(np.uint8).reshape(k // 512, 16, n))


def unpack_weight(words, scales, fmt):
    g, _, n = scales.shape
    words = np.ascontiguousarray(words).reshape(g, 128, n, -1)
    if fmt == "e4m3":
        vals = words.view(ml_dtypes.float8_e4m3fn).astype(np.float64)
    else:
        nib = np.empty((g, 128, n, 4), np.uint8)
        nib[..., 0::2] = words & 0xF
        nib[..., 1::2] = words >> 4
        vals = E2M1[nib]
    vals = vals * np.repeat(np.exp2(scales.astype(np.float64) - 127.0), 8, axis=1)[..., None]
    return vals.transpose(0, 1, 3, 2).reshape(g * 512, n)


def gelu(v):
    return 0.5 * v * (1.0 + np.tanh(np.sqrt(2.0 / np.pi) * (v + 0.044715 * v**3)))


def silu(v):
    return v / (1.0 + np.exp(-np.maximum(v, -700.0)))


K, T, E, C, H, N = 512, 1024, 8, 256, 512, 128


def by_expert(wq, xq):
    return np.concatenate([wq[e].T @ xq[:, e * C:(e + 1) * C] for e in range(E)], axis=1)


def setup_inputs():
    n = np.random.standard_normal
    s = mx_kscale(K)
    u = mx_kscale(H)
    first = np.random.permutation(np.repeat(np.arange(E), T // E))
    second = (first + 1 + np.random.permutation(np.repeat(np.arange(E - 1), -(-T // (E - 1)))[:T])) % E
    while np.bincount(second, minlength=E).max() != T // E:
        load = np.bincount(second, minlength=E); hi, lo = int(load.argmax()), int(load.argmin())
        t = np.flatnonzero((second == hi) & (first != lo))[0]; second[t] = lo
    slot_token = np.empty(E * C, np.int64); pos = np.empty((2, T), np.int64); fill = np.zeros(E, np.int64)
    place = np.stack([np.random.permutation(C) for _ in range(E)])
    for r, deal in enumerate((first, second)):
        for t in np.random.permutation(T):
            e = deal[t]; j = e * C + place[e, fill[e]]; fill[e] += 1; slot_token[j] = t; pos[r, t] = j
    g = np.random.uniform(0.2, 0.8, T)
    x = pack_weight(n((K, T)) * s[:, None], "e4m3")
    wg = pack_weight(n((K, N)) / np.sqrt(K) / s[:, None], "e2m1")
    return {
        "x_words": x[0],
        "x_scales": x[1],
        "wg_words": wg[0],
        "wg_scales": wg[1],
        "w1": (n((E, K, H)) / np.sqrt(K) / s[None, :, None] * u).astype(np.float32),
        "w2": (n((E, H, N)) / np.sqrt(H) / u[None, :, None]).astype(np.float32),
        "gate": np.stack([np.tile(g, (128, 1)), np.tile(1.0 - g, (128, 1))]).astype(np.float32),
        "offs": striped(slot_token),
        "pos1": striped(pos[0]),
        "pos2": striped(pos[1]),
    }


def reference(x_words, x_scales, wg_words, wg_scales, w1, w2, gate, offs, pos1, pos2):
    wg = unpack_weight(wg_words, wg_scales, "e2m1")
    w1q = mxq(f64(w1), 1, "e4m3")
    w2q = mxq(f64(w2), 1, "e4m3")
    idx = unstriped(offs)
    x = unpack_weight(x_words, x_scales, "e4m3")
    o = silu(wg.T @ x)
    h = gelu(by_expert(w1q, x[:, idx]))
    y = by_expert(w2q, mxq(h, 0, "e4m3"))
    c = sum(f64(gate[r, :1]) * y[:, unstriped(p)] for r, p in enumerate((pos1, pos2)))
    return o * c

@@ -1,0 +1,232 @@
+from contextlib import ExitStack
+
+import concourse.mybir as mybir
+
+K, T, E, C, H, N = 512, 1024, 8, 256, 512, 128
+SLOTS = E * C
+FLOPS = 2 * (K * N * T + SLOTS * K * H + SLOTS * H * N)
+
+F32 = mybir.dt.float32
+BF16 = mybir.dt.bfloat16
+I32 = mybir.dt.int32
+U32 = mybir.dt.uint32
+U16 = mybir.dt.uint16
+U8 = mybir.dt.uint8
+FP8X4 = mybir.dt.float8_e4m3fn_x4
+FP4X4 = mybir.dt.float4_e2m1fn_x4
+ACT = mybir.ActivationFunctionType
+ALU = mybir.AluOpType
+
+P = 128
+PACK = 4
+PIECE = 512
+GATHER_DEPTH = 4
+CAST = ("SS", "SS", "SS", "VV", "VV", "VS", "VV", "VS")
+CAST2 = "VVVV"
+YCOPY = "SSSV"
+HOLD_H = {0: "w1_raw2"}
+HOLD_Q = {4: "w1_bf6", 5: "w1_bf7"}
+SILU_FIRST = 0
+W2_AFTER = (3, 7, 7, 7)
+TOKEN_CUTS = ((0, 768), (768, 1024))
+
+
+def tile_moe_ogt_gelu_silu_kernel(
+    tc, x_words, x_scales, wg_words, wg_scales, w1, w2, gate, offs, pos1, pos2, out
+):
+    nc = tc.nc
+    with ExitStack() as ctx:
+        keep = ctx.enter_context(tc.tile_pool(name="keep", bufs=1))
+        ring = ctx.enter_context(tc.tile_pool(name="ring", bufs=2))
+        psum = ctx.enter_context(tc.psum_pool(name="psum", bufs=2))
+
+        offs_sb = keep.tile([P, SLOTS // 16], U16, name="offs_sb")
+        pos_sb = [keep.tile([P, T // 16], U16, name="pos%d_sb" % r) for r in range(2)]
+        x_w = keep.tile([P, T], I32, name="x_w", align_bytes=64)
+        x_s = keep.tile([P, T], U8, name="x_s", align_bytes=64)
+        wg_w = keep.tile([P, 2 * N], U8, name="wg_w", align_bytes=64)
+        wg_s = keep.tile([P, N], U8, name="wg_s", align_bytes=64)
+        w1_raw = [keep.tile([P, PACK, H], F32, name="w1_raw%d" % e, align_bytes=64) for e in range(E)]
+        w2_raw = [keep.tile([P, 2, PACK, N], F32, name="w2_raw%d" % a) for a in range(E // 2)]
+        gate_sb = [keep.tile([P, T], F32, name="gate%d_sb" % r) for r in range(2)]
+        y_sb = keep.tile([P, SLOTS], F32, name="y_sb")
+        o_sb = keep.tile([P, T], F32, name="o_sb")
+        warm = keep.tile([P, 8], F32, name="warm")
+        warm_out = keep.tile([P, 8], F32, name="warm_out")
+
+        nc.vector.memset(x_s[:].bitcast(I32), 0)
+        nc.vector.memset(wg_s[:].bitcast(I32), 0)
+        nc.vector.memset(warm[:], 0.0)
+        nc.scalar.activation(warm_out[:], warm[:], ACT.Silu if SILU_FIRST else ACT.Gelu_apprx_tanh)
+
+        def load_scale_rows(queue, plane, rows, r):
+            queue.dma_start(plane[:].bitcast(I32)[r:P:32, :], rows[0].bitcast(I32)[r:16:4, :])
+
+        def load_w1(e):
+            nc.sync.dma_start(w1_raw[e][:], w1[e].rearrange("(p j) c -> p j c", j=PACK))
+
+        def load_w2(a):
+            nc.sync.dma_start(
+                w2_raw[a][:].rearrange("p e j n -> p e (j n)"),
+                w2[2 * a : 2 * a + 2].rearrange("e (p j) n -> p e (j n)", j=PACK),
+            )
+
+        nc.sync.dma_start(offs_sb[:], offs)
+        nc.sync.dma_start(x_w[:], x_words[0].rearrange("p t d -> p (t d)").bitcast(I32))
+        for r in range(4):
+            load_scale_rows(nc.scalar, x_s, x_scales, r)
+        for e in range(E):
+            load_w1(e)
+            for a in range(E // 2):
+                if W2_AFTER[a] == e:
+                    load_w2(a)
+        nc.sync.dma_start(wg_w[:].bitcast(I32), wg_words[0].bitcast(I32))
+        for r in range(4):
+            load_scale_rows(nc.sync, wg_s, wg_scales, r)
+        nc.sync.dma_start(pos_sb[0][:], pos1)
+        nc.sync.dma_start(gate_sb[0][:], gate[0])
+        nc.sync.dma_start(pos_sb[1][:], pos2)
+        nc.sync.dma_start(gate_sb[1][:], gate[1])
+
+        def copy_on(engine, dst, src):
+            if engine == "V":
+                nc.vector.tensor_copy(dst, src)
+            else:
+                nc.scalar.copy(dst, src)
+
+        w1_bf, w1_q, w1_s, xg_w, xg_s, h_bf, h_q, h_s, w2_q, w2_s, y_ps = ({} for i in range(11))
+
+        def gather(g):
+            xg_w[g] = ring.tile([P, PIECE], U32, name="xg_w", align_bytes=64, bufs=GATHER_DEPTH)
+            xg_s[g] = ring.tile([P, PIECE], U8, name="xg_s", align_bytes=64, bufs=GATHER_DEPTH)
+            piece = offs_sb[:, g * PIECE // 16 : (g + 1) * PIECE // 16]
+            nc.vector.tensor_copy(xg_w[g][:], x_w[:].bitcast(U32).indirect(piece))
+            nc.vector.tensor_copy(xg_s[g][:], x_s[:].indirect(piece))
+
+        def round_w1(e):
+            w1_bf[e] = keep.tile([P, PACK * H], BF16, name="w1_bf%d" % e, align_bytes=64)
+            dst = w1_bf[e][:].rearrange("p (t m j) -> p m j t", t=PACK, j=PACK)
+            src = w1_raw[e][:].rearrange("p j (m t) -> p m j t", t=PACK)
+            copy_on(CAST[e][0], dst[:, :, :, 0:2], src[:, :, :, 0:2])
+            copy_on(CAST[e][1], dst[:, :, :, 2:4], src[:, :, :, 2:4])
+
+        def quantise_w1(e):
+            w1_q[e] = ring.tile([P, H], U32, name="w1_q", align_bytes=64, bufs=3)
+            w1_s[e] = ring.tile([P, H], U8, name="w1_s", align_bytes=64, bufs=3)
+            nc.vector.quantize_mx(out=w1_q[e][:].bitcast(FP8X4), scales=w1_s[e][:], in_=w1_bf[e][:])
+
+        def first_layer(e):
+            if e % 2 == 0:
+                pair = keep.tile([P, 2 * PACK * C], BF16, name="h_bf%d" % e, tag=HOLD_H.get(e // 2, "h_bf%d" % e), align_bytes=64)
+                h_bf[e] = pair[:, : PACK * C]
+                h_bf[e + 1] = pair[:, PACK * C :]
+            g, first = divmod(e * C, PIECE)
+            for u in range(2):
+                slots = slice(first + u * P, first + (u + 1) * P)
+                h_ps = psum.tile([P, PACK, P], F32, name="h_ps", tag="bank%d" % ((2 * e + u) % 4), bufs=1)
+                for t in range(PACK):
+                    cols = slice(t * P, (t + 1) * P)
+                    nc.tensor.matmul_mx(
+                        out=h_ps[:, t, :],
+                        lhsT=w1_q[e][:, cols].bitcast(FP8X4),
+                        lhsT_scale=w1_s[e][:, cols],
+                        rhs=xg_w[g][:, slots].bitcast(FP8X4),
+                        rhs_scale=xg_s[g][:, slots],
+                        start=True,
+                        stop=True,
+                    )
+                nc.scalar.activation(
+                    h_bf[e][:, u * PACK * P : (u + 1) * PACK * P].rearrange("p (n t) -> p n t", t=PACK),
+                    h_ps[:].rearrange("p t n -> p n t"),
+                    ACT.Gelu_apprx_tanh,
+                )
+
+        def quantise_h(e):
+            tag = HOLD_Q.get(e, "h_q%d" % e)
+            h_q[e] = keep.tile([P, C], U32, name="h_q%d" % e, tag=tag, align_bytes=64)
+            h_s[e] = keep.tile([P, C], U8, name="h_s%d" % e, align_bytes=64)
+            nc.vector.quantize_mx(out=h_q[e][:].bitcast(FP8X4), scales=h_s[e][:], in_=h_bf[e])
+
+        def prepare_w2(a):
+            w2_bf = ring.tile([P, 2 * PACK * N], BF16, name="w2_bf", align_bytes=64)
+            copy_on(
+                CAST2[a],
+                w2_bf[:].rearrange("p (e c i j) -> p e c j i", e=2, i=PACK, j=PACK),
+                w2_raw[a][:].rearrange("p e j (c i) -> p e c j i", i=PACK),
+            )
+            w2_q[a] = ring.tile([P, 2 * N], U32, name="w2_q", align_bytes=64)
+            w2_s[a] = ring.tile([P, 2 * N], U8, name="w2_s", align_bytes=64)
+            nc.vector.quantize_mx(out=w2_q[a][:].bitcast(FP8X4), scales=w2_s[a][:], in_=w2_bf[:])
+
+        def second_layer(e):
+            a, b = divmod(e, 2)
+            if b == 0:
+                y_ps[a] = psum.tile([P, 2 * C], F32, name="y_ps")
+            nc.tensor.matmul_mx(
+                out=y_ps[a][:, b * C : (b + 1) * C],
+                lhsT=w2_q[a][:, b * N : (b + 1) * N].bitcast(FP8X4),
+                lhsT_scale=w2_s[a][:, b * N : (b + 1) * N],
+                rhs=h_q[e][:].bitcast(FP8X4),
+                rhs_scale=h_s[e][:],
+                start=True,
+                stop=True,
+            )
+            if b == 1:
+                copy_on(YCOPY[a], y_sb[:, a * 2 * C : (a + 1) * 2 * C], y_ps[a][:])
+
+        def output_gate():
+            for u in range(2):
+                tokens = slice(u * 512, (u + 1) * 512)
+                o_ps = psum.tile([P, 512], F32, name="o_ps", tag="bank%d" % (3 - u), bufs=1)
+                nc.tensor.matmul_mx(
+                    out=o_ps[:],
+                    lhsT=wg_w[:].bitcast(FP4X4),
+                    lhsT_scale=wg_s[:],
+                    rhs=x_w[:, tokens].bitcast(FP8X4),
+                    rhs_scale=x_s[:, tokens],
+                    start=True,
+                    stop=True,
+                )
+                nc.scalar.activation(o_sb[:, tokens], o_ps[:], ACT.Silu)
+
+        if SILU_FIRST:
+            output_gate()
+            nc.scalar.activation(warm_out[:], o_sb[:, T - 8 :], ACT.Gelu_apprx_tanh)
+
+        for s in range(E + 2):
+            if s < E:
+                if s * C % PIECE == 0:
+                    gather(s * C // PIECE)
+                round_w1(s)
+                quantise_w1(s)
+            if 1 <= s <= E:
+                first_layer(s - 1)
+            if 2 <= s:
+                quantise_h(s - 2)
+                if s % 2 == 0:
+                    prepare_w2(s // 2 - 1)
+                second_layer(s - 2)
+
+        if not SILU_FIRST:
+            output_gate()
+        else:
+            for r in range(2):
+                og = keep.tile([P, T], F32, name="og%d" % r)
+                nc.vector.tensor_tensor(og[:], gate_sb[r][:], o_sb[:], ALU.mult)
+                gate_sb[r] = og
+
+        for c, (t0, t1) in enumerate(TOKEN_CUTS):
+            parts = []
+            for r in range(2):
+                part = keep.tile([P, t1 - t0], F32, name="part%d_%d" % (c, r))
+                nc.vector.tensor_tensor(
+                    part[:], y_sb[:].indirect(pos_sb[r][:, t0 // 16 : t1 // 16]), gate_sb[r][:, t0:t1], ALU.mult
+                )
+                parts.append(part)
+            total = keep.tile([P, t1 - t0], F32, name="total%d" % c)
+            nc.vector.tensor_tensor(total[:], parts[0][:], parts[1][:], ALU.add)
+            result = total
+            if not SILU_FIRST:
+                result = keep.tile([P, t1 - t0], F32, name="result%d" % c)
+                nc.vector.tensor_tensor(result[:], total[:], o_sb[:, t0:t1], ALU.mult)
+            nc.sync.dma_start(out[:, t0:t1], result[:])

@@ -21,13 +21,17 @@ P = 128
 PACK = 4
 PIECE = 512
 GATHER_DEPTH = 4
-CAST = ("SS", "SS", "SS", "VV", "VV", "VS", "VV", "VS")
+CAST = ("SS", "SS", "SS", "SS", "VV", "VV", "VS", "VS")
 CAST2 = "VVVV"
 YCOPY = "SSSV"
-HOLD_H = {0: "w1_raw2"}
-HOLD_Q = {4: "w1_bf6", 5: "w1_bf7"}
+HOLD_H = {0: "w1_raw3"}
+HOLD_Q = {0: "w1_bf3", 1: "w1_bf4", 2: "w1_bf5", 3: "w1_bf6", 4: "w1_bf7"}
 SILU_FIRST = 0
-W2_AFTER = (3, 7, 7, 7)
+HOLD_W = {3: "w1_raw4", 4: "w1_raw5"}
+LAG_H = 1
+LAG_Q = 4
+SPLIT_Y = "VV"
+LOADS = "a0 x wg a1 s0 s1 a2 s2 s3 a3 p0 p1 a4 b0 a5 a6 b1 a7 b2 b3 g0 g1"
 TOKEN_CUTS = ((0, 768), (768, 1024))
 
 
@@ -57,7 +61,6 @@ def tile_moe_ogt_gelu_silu_kernel(
         nc.vector.memset(x_s[:].bitcast(I32), 0)
         nc.vector.memset(wg_s[:].bitcast(I32), 0)
         nc.vector.memset(warm[:], 0.0)
-        nc.scalar.activation(warm_out[:], warm[:], ACT.Silu if SILU_FIRST else ACT.Gelu_apprx_tanh)
 
         def load_scale_rows(queue, plane, rows, r):
             queue.dma_start(plane[:].bitcast(I32)[r:P:32, :], rows[0].bitcast(I32)[r:16:4, :])
@@ -71,22 +74,27 @@ def tile_moe_ogt_gelu_silu_kernel(
                 w2[2 * a : 2 * a + 2].rearrange("e (p j) n -> p e (j n)", j=PACK),
             )
 
+        loads = {
+            "x": lambda: nc.sync.dma_start(x_w[:], x_words[0].rearrange("p t d -> p (t d)").bitcast(I32)),
+            "wg": lambda: nc.sync.dma_start(wg_w[:].bitcast(I32), wg_words[0].bitcast(I32)),
+            "p0": lambda: nc.sync.dma_start(pos_sb[0][:], pos1),
+            "p1": lambda: nc.sync.dma_start(pos_sb[1][:], pos2),
+            "g0": lambda: nc.sync.dma_start(gate_sb[0][:], gate[0]),
+            "g1": lambda: nc.sync.dma_start(gate_sb[1][:], gate[1]),
+        }
         nc.sync.dma_start(offs_sb[:], offs)
-        nc.sync.dma_start(x_w[:], x_words[0].rearrange("p t d -> p (t d)").bitcast(I32))
         for r in range(4):
             load_scale_rows(nc.scalar, x_s, x_scales, r)
-        for e in range(E):
-            load_w1(e)
-            for a in range(E // 2):
-                if W2_AFTER[a] == e:
-                    load_w2(a)
-        nc.sync.dma_start(wg_w[:].bitcast(I32), wg_words[0].bitcast(I32))
-        for r in range(4):
-            load_scale_rows(nc.sync, wg_s, wg_scales, r)
-        nc.sync.dma_start(pos_sb[0][:], pos1)
-        nc.sync.dma_start(gate_sb[0][:], gate[0])
-        nc.sync.dma_start(pos_sb[1][:], pos2)
-        nc.sync.dma_start(gate_sb[1][:], gate[1])
+        nc.scalar.activation(warm_out[:], warm[:], ACT.Silu if SILU_FIRST else ACT.Gelu_apprx_tanh)
+        for what in LOADS.split():
+            if what in loads:
+                loads[what]()
+            elif what[0] == "s":
+                load_scale_rows(nc.sync, wg_s, wg_scales, int(what[1]))
+            elif what[0] == "a":
+                load_w1(int(what[1]))
+            else:
+                load_w2(int(what[1]))
 
         def copy_on(engine, dst, src):
             if engine == "V":
@@ -111,8 +119,8 @@ def tile_moe_ogt_gelu_silu_kernel(
             copy_on(CAST[e][1], dst[:, :, :, 2:4], src[:, :, :, 2:4])
 
         def quantise_w1(e):
-            w1_q[e] = ring.tile([P, H], U32, name="w1_q", align_bytes=64, bufs=3)
-            w1_s[e] = ring.tile([P, H], U8, name="w1_s", align_bytes=64, bufs=3)
+            w1_q[e] = keep.tile([P, H], U32, name="w1_q%d" % e, tag=HOLD_W.get(e, "w1_q%d" % e), align_bytes=64)
+            w1_s[e] = keep.tile([P, H], U8, name="w1_s%d" % e, align_bytes=64)
             nc.vector.quantize_mx(out=w1_q[e][:].bitcast(FP8X4), scales=w1_s[e][:], in_=w1_bf[e][:])
 
         def first_layer(e):
@@ -160,7 +168,8 @@ def tile_moe_ogt_gelu_silu_kernel(
 
         def second_layer(e):
             a, b = divmod(e, 2)
-            if b == 0:
+            alone = e >= E - 2 and SPLIT_Y
+            if b == 0 or alone:
                 y_ps[a] = psum.tile([P, 2 * C], F32, name="y_ps")
             nc.tensor.matmul_mx(
                 out=y_ps[a][:, b * C : (b + 1) * C],
@@ -171,7 +180,9 @@ def tile_moe_ogt_gelu_silu_kernel(
                 start=True,
                 stop=True,
             )
-            if b == 1:
+            if alone:
+                copy_on(SPLIT_Y[b], y_sb[:, e * C : (e + 1) * C], y_ps[a][:, b * C : (b + 1) * C])
+            elif b == 1:
                 copy_on(YCOPY[a], y_sb[:, a * 2 * C : (a + 1) * 2 * C], y_ps[a][:])
 
         def output_gate():
@@ -193,19 +204,20 @@ def tile_moe_ogt_gelu_silu_kernel(
             output_gate()
             nc.scalar.activation(warm_out[:], o_sb[:, T - 8 :], ACT.Gelu_apprx_tanh)
 
-        for s in range(E + 2):
+        for s in range(E + LAG_Q):
             if s < E:
                 if s * C % PIECE == 0:
                     gather(s * C // PIECE)
                 round_w1(s)
-                quantise_w1(s)
             if 1 <= s <= E:
-                first_layer(s - 1)
-            if 2 <= s:
-                quantise_h(s - 2)
-                if s % 2 == 0:
-                    prepare_w2(s // 2 - 1)
-                second_layer(s - 2)
+                quantise_w1(s - 1)
+            if 0 <= s - LAG_H < E:
+                first_layer(s - LAG_H)
+            if 0 <= s - LAG_Q < E:
+                quantise_h(s - LAG_Q)
+                if (s - LAG_Q) % 2 == 0:
+                    prepare_w2((s - LAG_Q) // 2)
+                second_layer(s - LAG_Q)
 
         if not SILU_FIRST:
             output_gate()

@@ -1,6 +1,7 @@
 from contextlib import ExitStack
 
 import concourse.mybir as mybir
+from concourse.masks import make_identity
 
 K, T, E, C, H, N = 512, 1024, 8, 256, 512, 128
 SLOTS = E * C
@@ -21,18 +22,21 @@ P = 128
 PACK = 4
 PIECE = 512
 GATHER_DEPTH = 4
-CAST = ("SS", "SS", "SS", "SS", "VV", "VV", "VS", "VS")
-CAST2 = "VVVV"
+CAST = ("SS", "SS", "SS", "SS", "VV", "VV", "VS", "VV")
+CAST2 = "VSVV"
 YCOPY = "SSSV"
 HOLD_H = {0: "w1_raw3"}
 HOLD_Q = {0: "w1_bf3", 1: "w1_bf4", 2: "w1_bf5", 3: "w1_bf6", 4: "w1_bf7"}
-SILU_FIRST = 0
+CHUNK = 256
+LATE = 0
+TURNED = 512
+WHOLE = 1
+CUTS = (512, 768, 1024)
 HOLD_W = {3: "w1_raw4", 4: "w1_raw5"}
 LAG_H = 1
 LAG_Q = 4
 SPLIT_Y = "VV"
-LOADS = "a0 x wg a1 s0 s1 a2 s2 s3 a3 p0 p1 a4 b0 a5 a6 b1 a7 b2 b3 g0 g1"
-TOKEN_CUTS = ((0, 768), (768, 1024))
+LOADS = "x a0 a1 a2 a3 a4 b0 a5 a6 a7 b1 b2 b3 wg s0 s1 s2 s3 g0 g1 p0 p1 h0 h1"
 
 
 def tile_moe_ogt_gelu_silu_kernel(
@@ -52,7 +56,11 @@ def tile_moe_ogt_gelu_silu_kernel(
         wg_s = keep.tile([P, N], U8, name="wg_s", align_bytes=64)
         w1_raw = [keep.tile([P, PACK, H], F32, name="w1_raw%d" % e, align_bytes=64) for e in range(E)]
         w2_raw = [keep.tile([P, 2, PACK, N], F32, name="w2_raw%d" % a) for a in range(E // 2)]
-        gate_sb = [keep.tile([P, T], F32, name="gate%d_sb" % r) for r in range(2)]
+        gate_rows = keep.tile([P, P], F32, name="gate_rows")
+        gate_cols = keep.tile([P, 2 * T // P], F32, name="gate_cols")
+        gate_sb = [keep.tile([P, T - TURNED], F32, name="gate%d_sb" % r) for r in range(2)]
+        ident = keep.tile([P, P], F32, name="ident")
+        make_identity(nc, ident[:])
         y_sb = keep.tile([P, SLOTS], F32, name="y_sb")
         o_sb = keep.tile([P, T], F32, name="o_sb")
         warm = keep.tile([P, 8], F32, name="warm")
@@ -61,6 +69,7 @@ def tile_moe_ogt_gelu_silu_kernel(
         nc.vector.memset(x_s[:].bitcast(I32), 0)
         nc.vector.memset(wg_s[:].bitcast(I32), 0)
         nc.vector.memset(warm[:], 0.0)
+        nc.vector.memset(gate_rows[:], 0.0)
 
         def load_scale_rows(queue, plane, rows, r):
             queue.dma_start(plane[:].bitcast(I32)[r:P:32, :], rows[0].bitcast(I32)[r:16:4, :])
@@ -79,13 +88,15 @@ def tile_moe_ogt_gelu_silu_kernel(
             "wg": lambda: nc.sync.dma_start(wg_w[:].bitcast(I32), wg_words[0].bitcast(I32)),
             "p0": lambda: nc.sync.dma_start(pos_sb[0][:], pos1),
             "p1": lambda: nc.sync.dma_start(pos_sb[1][:], pos2),
-            "g0": lambda: nc.sync.dma_start(gate_sb[0][:], gate[0]),
-            "g1": lambda: nc.sync.dma_start(gate_sb[1][:], gate[1]),
+            "h0": lambda: nc.sync.dma_start(gate_sb[0][:], gate[0][:, TURNED:]),
+            "h1": lambda: nc.sync.dma_start(gate_sb[1][:], gate[1][:, TURNED:]),
+            "g0": lambda: nc.sync.dma_start(gate_rows[0:8, :], gate[0, 0].rearrange("(c q) -> c q", q=P)),
+            "g1": lambda: nc.sync.dma_start(gate_rows[8:16, :], gate[1, 0].rearrange("(c q) -> c q", q=P)),
         }
         nc.sync.dma_start(offs_sb[:], offs)
         for r in range(4):
             load_scale_rows(nc.scalar, x_s, x_scales, r)
-        nc.scalar.activation(warm_out[:], warm[:], ACT.Silu if SILU_FIRST else ACT.Gelu_apprx_tanh)
+        nc.scalar.activation(warm_out[:], warm[:], ACT.Gelu_apprx_tanh)
         for what in LOADS.split():
             if what in loads:
                 loads[what]()
@@ -115,8 +126,11 @@ def tile_moe_ogt_gelu_silu_kernel(
             w1_bf[e] = keep.tile([P, PACK * H], BF16, name="w1_bf%d" % e, align_bytes=64)
             dst = w1_bf[e][:].rearrange("p (t m j) -> p m j t", t=PACK, j=PACK)
             src = w1_raw[e][:].rearrange("p j (m t) -> p m j t", t=PACK)
-            copy_on(CAST[e][0], dst[:, :, :, 0:2], src[:, :, :, 0:2])
-            copy_on(CAST[e][1], dst[:, :, :, 2:4], src[:, :, :, 2:4])
+            if CAST[e][0] == CAST[e][1] and WHOLE:
+                copy_on(CAST[e][0], dst, src)
+            else:
+                copy_on(CAST[e][0], dst[:, :, :, 0:2], src[:, :, :, 0:2])
+                copy_on(CAST[e][1], dst[:, :, :, 2:4], src[:, :, :, 2:4])
 
         def quantise_w1(e):
             w1_q[e] = keep.tile([P, H], U32, name="w1_q%d" % e, tag=HOLD_W.get(e, "w1_q%d" % e), align_bytes=64)
@@ -200,9 +214,9 @@ def tile_moe_ogt_gelu_silu_kernel(
                 )
                 nc.scalar.activation(o_sb[:, tokens], o_ps[:], ACT.Silu)
 
-        if SILU_FIRST:
-            output_gate()
-            nc.scalar.activation(warm_out[:], o_sb[:, T - 8 :], ACT.Gelu_apprx_tanh)
+        gate_ps = psum.tile([P, P], F32, name="gate_ps", tag="total")
+        nc.tensor.transpose(gate_ps[:], gate_rows[:], ident[:])
+        nc.scalar.copy(gate_cols[:], gate_ps[:, : 2 * T // P])
 
         for s in range(E + LAG_Q):
             if s < E:
@@ -219,26 +233,60 @@ def tile_moe_ogt_gelu_silu_kernel(
                     prepare_w2((s - LAG_Q) // 2)
                 second_layer(s - LAG_Q)
 
-        if not SILU_FIRST:
-            output_gate()
-        else:
-            for r in range(2):
-                og = keep.tile([P, T], F32, name="og%d" % r)
-                nc.vector.tensor_tensor(og[:], gate_sb[r][:], o_sb[:], ALU.mult)
-                gate_sb[r] = og
+        output_gate()
 
-        for c, (t0, t1) in enumerate(TOKEN_CUTS):
+        totals = []
+        for c in range(TURNED // CHUNK):
+            tokens = slice(c * CHUNK, (c + 1) * CHUNK)
+            scaled = ring.tile([P, 2, CHUNK], F32, name="scaled")
+            for r in range(2):
+                picked = ring.tile([P, CHUNK], F32, name="picked", bufs=4)
+                nc.vector.tensor_copy(picked[:], y_sb[:].indirect(pos_sb[r][:, c * CHUNK // 16 : (c + 1) * CHUNK // 16]))
+                if c % 2 == 0:
+                    turned = psum.tile([P, CHUNK], F32, name="turned", tag="bank%d" % r, bufs=1)
+                else:
+                    turned = psum.tile([P, CHUNK], F32, name="turned", tag="y_ps")
+                for b in range(CHUNK // P):
+                    cols = slice(b * P, (b + 1) * P)
+                    nc.tensor.transpose(turned[:, cols], picked[:, cols], ident[:])
+                for b in range(CHUNK // P):
+                    cols = slice(b * P, (b + 1) * P)
+                    g = r * (T // P) + c * (CHUNK // P) + b
+                    nc.scalar.activation(scaled[:, r, cols], turned[:, cols], ACT.Copy, scale=gate_cols[:, g : g + 1])
+            total = psum.tile([P, CHUNK], F32, name="total")
+            for b in range(CHUNK // P):
+                cols = slice(b * P, (b + 1) * P)
+                for r in range(2):
+                    nc.tensor.matmul(
+                        total[:, cols], scaled[:, r, cols], ident[:], is_transpose=True, start=(r == 0), stop=(r == 1)
+                    )
+            totals.append(total)
+
+        def finish_turned(c):
+            tokens = slice(c * CHUNK, (c + 1) * CHUNK)
+            result = keep.tile([P, CHUNK], F32, name="result%d" % c)
+            nc.vector.tensor_tensor(result[:], totals[c][:], o_sb[:, tokens], ALU.mult)
+            nc.sync.dma_start(out[:, tokens], result[:])
+
+        if not LATE:
+            for c in range(TURNED // CHUNK):
+                finish_turned(c)
+        for t0, t1 in zip(CUTS[:-1], CUTS[1:]):
             parts = []
             for r in range(2):
-                part = keep.tile([P, t1 - t0], F32, name="part%d_%d" % (c, r))
+                part = keep.tile([P, t1 - t0], F32, name="part%d_%d" % (t0, r))
                 nc.vector.tensor_tensor(
-                    part[:], y_sb[:].indirect(pos_sb[r][:, t0 // 16 : t1 // 16]), gate_sb[r][:, t0:t1], ALU.mult
+                    part[:],
+                    y_sb[:].indirect(pos_sb[r][:, t0 // 16 : t1 // 16]),
+                    gate_sb[r][:, t0 - TURNED : t1 - TURNED],
+                    ALU.mult,
                 )
                 parts.append(part)
-            total = keep.tile([P, t1 - t0], F32, name="total%d" % c)
-            nc.vector.tensor_tensor(total[:], parts[0][:], parts[1][:], ALU.add)
-            result = total
-            if not SILU_FIRST:
-                result = keep.tile([P, t1 - t0], F32, name="result%d" % c)
-                nc.vector.tensor_tensor(result[:], total[:], o_sb[:, t0:t1], ALU.mult)
-            nc.sync.dma_start(out[:, t0:t1], result[:])
+            both = keep.tile([P, t1 - t0], F32, name="both%d" % t0)
+            nc.vector.tensor_tensor(both[:], parts[0][:], parts[1][:], ALU.add)
+            gated = keep.tile([P, t1 - t0], F32, name="gated%d" % t0)
+            nc.vector.tensor_tensor(gated[:], both[:], o_sb[:, t0:t1], ALU.mult)
+            nc.sync.dma_start(out[:, t0:t1], gated[:])
+        if LATE:
+            for c in range(TURNED // CHUNK):
+                finish_turned(c)

@@ -21,22 +21,24 @@ ALU = mybir.AluOpType
 P = 128
 PACK = 4
 PIECE = 512
-GATHER_DEPTH = 4
-CAST = ("SS", "SS", "SS", "SS", "VV", "VV", "VS", "VV")
-CAST2 = "VSVV"
+HOLD_R = {2: 5, 3: 6, 4: 6, 5: 7}
+RAW = PACK * H * 4
+HOLD_X = {2: "w1_bf0", 3: "w1_bf1"}
+CAST = ("SS","SS","SS","VV","SS","VV","VV","VS")
+CAST2 = "VVVV"
 YCOPY = "SSSV"
-HOLD_H = {0: "w1_raw3"}
-HOLD_Q = {0: "w1_bf3", 1: "w1_bf4", 2: "w1_bf5", 3: "w1_bf6", 4: "w1_bf7"}
+HOLD_H = {0: 1, 1: 2, 2: 4, 3: 4, 6: 7}
+HOLD_Q = {}
 CHUNK = 256
 LATE = 0
 TURNED = 512
 WHOLE = 1
 CUTS = (512, 768, 1024)
-HOLD_W = {3: "w1_raw4", 4: "w1_raw5"}
-LAG_H = 1
-LAG_Q = 4
+HOLD_W = {2: 3}
+LAG_H = 2
+LAG_Q = 3
 SPLIT_Y = "VV"
-LOADS = "x a0 a1 a2 a3 a4 b0 a5 a6 a7 b1 b2 b3 wg s0 s1 s2 s3 g0 g1 p0 p1 h0 h1"
+LOADS = "a0 a1 x a2 a3 a4 b0 a5 a6 a7 b1 b2 b3 wg s0 s1 s2 s3 g0 g1 p0 p1 h0 h1"
 
 
 def tile_moe_ogt_gelu_silu_kernel(
@@ -45,6 +47,7 @@ def tile_moe_ogt_gelu_silu_kernel(
     nc = tc.nc
     with ExitStack() as ctx:
         keep = ctx.enter_context(tc.tile_pool(name="keep", bufs=1))
+        reuse = ctx.enter_context(tc.tile_pool(name="reuse", bufs=1))
         ring = ctx.enter_context(tc.tile_pool(name="ring", bufs=2))
         psum = ctx.enter_context(tc.psum_pool(name="psum", bufs=2))
 
@@ -54,7 +57,7 @@ def tile_moe_ogt_gelu_silu_kernel(
         x_s = keep.tile([P, T], U8, name="x_s", align_bytes=64)
         wg_w = keep.tile([P, 2 * N], U8, name="wg_w", align_bytes=64)
         wg_s = keep.tile([P, N], U8, name="wg_s", align_bytes=64)
-        w1_raw = [keep.tile([P, PACK, H], F32, name="w1_raw%d" % e, align_bytes=64) for e in range(E)]
+        w1_raw = [reuse.tile([P, PACK, H], F32, name="w1_raw%d" % e, align_bytes=64, offset=e * RAW) for e in range(E)]
         w2_raw = [keep.tile([P, 2, PACK, N], F32, name="w2_raw%d" % a) for a in range(E // 2)]
         gate_rows = keep.tile([P, P], F32, name="gate_rows")
         gate_cols = keep.tile([P, 2 * T // P], F32, name="gate_cols")
@@ -66,7 +69,6 @@ def tile_moe_ogt_gelu_silu_kernel(
         warm = keep.tile([P, 8], F32, name="warm")
         warm_out = keep.tile([P, 8], F32, name="warm_out")
 
-        nc.vector.memset(x_s[:].bitcast(I32), 0)
         nc.vector.memset(wg_s[:].bitcast(I32), 0)
         nc.vector.memset(warm[:], 0.0)
         nc.vector.memset(gate_rows[:], 0.0)
@@ -94,8 +96,11 @@ def tile_moe_ogt_gelu_silu_kernel(
             "g1": lambda: nc.sync.dma_start(gate_rows[8:16, :], gate[1, 0].rearrange("(c q) -> c q", q=P)),
         }
         nc.sync.dma_start(offs_sb[:], offs)
-        for r in range(4):
-            load_scale_rows(nc.scalar, x_s, x_scales, r)
+        for q in range(4):
+            nc.sync.dma_start(
+                x_s[:].bitcast(I32)[32 * q : 32 * q + 32, :],
+                x_scales[0].bitcast(I32)[4 * q : 4 * q + 4, :].partition_broadcast(8),
+            )
         nc.scalar.activation(warm_out[:], warm[:], ACT.Gelu_apprx_tanh)
         for what in LOADS.split():
             if what in loads:
@@ -116,11 +121,14 @@ def tile_moe_ogt_gelu_silu_kernel(
         w1_bf, w1_q, w1_s, xg_w, xg_s, h_bf, h_q, h_s, w2_q, w2_s, y_ps = ({} for i in range(11))
 
         def gather(g):
-            xg_w[g] = ring.tile([P, PIECE], U32, name="xg_w", align_bytes=64, bufs=GATHER_DEPTH)
-            xg_s[g] = ring.tile([P, PIECE], U8, name="xg_s", align_bytes=64, bufs=GATHER_DEPTH)
+            xg_w[g] = keep.tile([P, PIECE], U32, name="xg_w%d" % g, tag=HOLD_X.get(g, "xg_w%d" % g), align_bytes=64)
+            xg_s[g] = keep.tile([P, PIECE], U8, name="xg_s%d" % g, align_bytes=64)
             piece = offs_sb[:, g * PIECE // 16 : (g + 1) * PIECE // 16]
-            nc.vector.tensor_copy(xg_w[g][:], x_w[:].bitcast(U32).indirect(piece))
             nc.vector.tensor_copy(xg_s[g][:], x_s[:].indirect(piece))
+            for u in range(2):
+                nc.vector.tensor_copy(
+                    xg_w[g][:, u * C : (u + 1) * C], x_w[:].bitcast(U32).indirect(piece[:, u * C // 16 : (u + 1) * C // 16])
+                )
 
         def round_w1(e):
             w1_bf[e] = keep.tile([P, PACK * H], BF16, name="w1_bf%d" % e, align_bytes=64)
@@ -133,15 +141,20 @@ def tile_moe_ogt_gelu_silu_kernel(
                 copy_on(CAST[e][1], dst[:, :, :, 2:4], src[:, :, :, 2:4])
 
         def quantise_w1(e):
-            w1_q[e] = keep.tile([P, H], U32, name="w1_q%d" % e, tag=HOLD_W.get(e, "w1_q%d" % e), align_bytes=64)
+            if e in HOLD_W:
+                w1_q[e] = reuse.tile([P, H], U32, name="w1_q%d" % e, align_bytes=64, offset=HOLD_W[e] * RAW + 4096)
+            else:
+                w1_q[e] = keep.tile([P, H], U32, name="w1_q%d" % e, align_bytes=64)
             w1_s[e] = keep.tile([P, H], U8, name="w1_s%d" % e, align_bytes=64)
             nc.vector.quantize_mx(out=w1_q[e][:].bitcast(FP8X4), scales=w1_s[e][:], in_=w1_bf[e][:])
 
         def first_layer(e):
-            if e % 2 == 0:
-                pair = keep.tile([P, 2 * PACK * C], BF16, name="h_bf%d" % e, tag=HOLD_H.get(e // 2, "h_bf%d" % e), align_bytes=64)
-                h_bf[e] = pair[:, : PACK * C]
-                h_bf[e + 1] = pair[:, PACK * C :]
+            if e in HOLD_H:
+                h_bf[e] = reuse.tile(
+                    [P, PACK * C], BF16, name="h_bf%d" % e, align_bytes=64, offset=HOLD_H[e] * RAW + e % 2 * 2048
+                )
+            else:
+                h_bf[e] = keep.tile([P, PACK * C], BF16, name="h_bf%d" % e, align_bytes=64)
             g, first = divmod(e * C, PIECE)
             for u in range(2):
                 slots = slice(first + u * P, first + (u + 1) * P)
@@ -164,10 +177,12 @@ def tile_moe_ogt_gelu_silu_kernel(
                 )
 
         def quantise_h(e):
-            tag = HOLD_Q.get(e, "h_q%d" % e)
-            h_q[e] = keep.tile([P, C], U32, name="h_q%d" % e, tag=tag, align_bytes=64)
+            if e in HOLD_R:
+                h_q[e] = reuse.tile([P, C], U32, name="h_q%d" % e, align_bytes=64, offset=HOLD_R[e] * RAW + 6144 + e % 2 * 1024)
+            else:
+                h_q[e] = keep.tile([P, C], U32, name="h_q%d" % e, tag=HOLD_Q.get(e, "h_q%d" % e), align_bytes=64)
             h_s[e] = keep.tile([P, C], U8, name="h_s%d" % e, align_bytes=64)
-            nc.vector.quantize_mx(out=h_q[e][:].bitcast(FP8X4), scales=h_s[e][:], in_=h_bf[e])
+            nc.vector.quantize_mx(out=h_q[e][:].bitcast(FP8X4), scales=h_s[e][:], in_=h_bf[e][:])
 
         def prepare_w2(a):
             w2_bf = ring.tile([P, 2 * PACK * N], BF16, name="w2_bf", align_bytes=64)

@@ -22,23 +22,26 @@ P = 128
 PACK = 4
 PIECE = 512
 HOLD_R = {2: 5, 3: 6, 4: 6, 5: 7}
+HALF_Q = 1
+FINE = 1
+SIDE = 1
+Y_BANK = {0: (4,), 2: (5,), 4: (0,), 6: (1,), 7: (4, 2)}
+PAIR0_AFTER = 3
 RAW = PACK * H * 4
 HOLD_X = {2: "w1_bf0", 3: "w1_bf1"}
 CAST = ("SS","SS","SS","VV","SS","VV","VV","VS")
-CAST2 = "VVVV"
+CAST2 = ("VV","VV","SV","VV")
 YCOPY = "SSSV"
-HOLD_H = {0: 1, 1: 2, 2: 4, 3: 4, 6: 7}
-HOLD_Q = {}
+HOLD_H = {0: 1, 1: 2, 2: 4, 3: 4, 5: 6, 6: 7}
+HOLD_Q = {7: "w2_bf3"}
 CHUNK = 256
-LATE = 0
+LATE = 1
 TURNED = 512
 WHOLE = 1
-CUTS = (512, 768, 1024)
+CUTS = {512: (512, 768, 1024), 768: (768, 1024), 256: (256, 512, 768, 1024)}
 HOLD_W = {2: 3}
-LAG_H = 2
-LAG_Q = 3
-SPLIT_Y = "VV"
-LOADS = "a0 a1 x a2 a3 a4 b0 a5 a6 a7 b1 b2 b3 wg s0 s1 s2 s3 g0 g1 p0 p1 h0 h1"
+SPLIT_Y = "SV"
+LOADS = "a0 a1 x a2 a3 a4 b0 a5 a6 a7 b1 b2 b3 wg s0 s1 s2 s3 g p0 p1 h0 h1"
 
 
 def tile_moe_ogt_gelu_silu_kernel(
@@ -58,20 +61,21 @@ def tile_moe_ogt_gelu_silu_kernel(
         wg_w = keep.tile([P, 2 * N], U8, name="wg_w", align_bytes=64)
         wg_s = keep.tile([P, N], U8, name="wg_s", align_bytes=64)
         w1_raw = [reuse.tile([P, PACK, H], F32, name="w1_raw%d" % e, align_bytes=64, offset=e * RAW) for e in range(E)]
-        w2_raw = [keep.tile([P, 2, PACK, N], F32, name="w2_raw%d" % a) for a in range(E // 2)]
+        w2_raw = [keep.tile([P, 2, PACK, N], F32, name="w2_raw%d" % a, align_bytes=64) for a in range(E // 2)]
         gate_rows = keep.tile([P, P], F32, name="gate_rows")
         gate_cols = keep.tile([P, 2 * T // P], F32, name="gate_cols")
         gate_sb = [keep.tile([P, T - TURNED], F32, name="gate%d_sb" % r) for r in range(2)]
         ident = keep.tile([P, P], F32, name="ident")
         make_identity(nc, ident[:])
         y_sb = keep.tile([P, SLOTS], F32, name="y_sb")
-        o_sb = keep.tile([P, T], F32, name="o_sb")
         warm = keep.tile([P, 8], F32, name="warm")
         warm_out = keep.tile([P, 8], F32, name="warm_out")
 
         nc.vector.memset(wg_s[:].bitcast(I32), 0)
         nc.vector.memset(warm[:], 0.0)
         nc.vector.memset(gate_rows[:], 0.0)
+
+        side = nc.sync
 
         def load_scale_rows(queue, plane, rows, r):
             queue.dma_start(plane[:].bitcast(I32)[r:P:32, :], rows[0].bitcast(I32)[r:16:4, :])
@@ -87,13 +91,12 @@ def tile_moe_ogt_gelu_silu_kernel(
 
         loads = {
             "x": lambda: nc.sync.dma_start(x_w[:], x_words[0].rearrange("p t d -> p (t d)").bitcast(I32)),
-            "wg": lambda: nc.sync.dma_start(wg_w[:].bitcast(I32), wg_words[0].bitcast(I32)),
+            "wg": lambda: side.dma_start(wg_w[:].bitcast(I32), wg_words[0].bitcast(I32)),
             "p0": lambda: nc.sync.dma_start(pos_sb[0][:], pos1),
             "p1": lambda: nc.sync.dma_start(pos_sb[1][:], pos2),
             "h0": lambda: nc.sync.dma_start(gate_sb[0][:], gate[0][:, TURNED:]),
             "h1": lambda: nc.sync.dma_start(gate_sb[1][:], gate[1][:, TURNED:]),
-            "g0": lambda: nc.sync.dma_start(gate_rows[0:8, :], gate[0, 0].rearrange("(c q) -> c q", q=P)),
-            "g1": lambda: nc.sync.dma_start(gate_rows[8:16, :], gate[1, 0].rearrange("(c q) -> c q", q=P)),
+            "g": lambda: side.dma_start(gate_rows[0:16, :], gate[:, 0, :].rearrange("r (c q) -> r c q", q=P)),
         }
         nc.sync.dma_start(offs_sb[:], offs)
         for q in range(4):
@@ -106,7 +109,7 @@ def tile_moe_ogt_gelu_silu_kernel(
             if what in loads:
                 loads[what]()
             elif what[0] == "s":
-                load_scale_rows(nc.sync, wg_s, wg_scales, int(what[1]))
+                load_scale_rows(side, wg_s, wg_scales, int(what[1]))
             elif what[0] == "a":
                 load_w1(int(what[1]))
             else:
@@ -118,7 +121,7 @@ def tile_moe_ogt_gelu_silu_kernel(
             else:
                 nc.scalar.copy(dst, src)
 
-        w1_bf, w1_q, w1_s, xg_w, xg_s, h_bf, h_q, h_s, w2_q, w2_s, y_ps = ({} for i in range(11))
+        w1_bf, w1_q, w1_s, xg_w, xg_s, h_bf, h_q, h_s, w2_bf, w2_q, w2_s, y_ps = ({} for i in range(12))
 
         def gather(g):
             xg_w[g] = keep.tile([P, PIECE], U32, name="xg_w%d" % g, tag=HOLD_X.get(g, "xg_w%d" % g), align_bytes=64)
@@ -146,7 +149,14 @@ def tile_moe_ogt_gelu_silu_kernel(
             else:
                 w1_q[e] = keep.tile([P, H], U32, name="w1_q%d" % e, align_bytes=64)
             w1_s[e] = keep.tile([P, H], U8, name="w1_s%d" % e, align_bytes=64)
-            nc.vector.quantize_mx(out=w1_q[e][:].bitcast(FP8X4), scales=w1_s[e][:], in_=w1_bf[e][:])
+            if CAST[e] == "VS" and HALF_Q:
+                for u in range(2):
+                    cols = slice(u * H // 2, (u + 1) * H // 2)
+                    nc.vector.quantize_mx(
+                        out=w1_q[e][:, cols].bitcast(FP8X4), scales=w1_s[e][:, cols], in_=w1_bf[e][:, u * 2 * H : (u + 1) * 2 * H]
+                    )
+            else:
+                nc.vector.quantize_mx(out=w1_q[e][:].bitcast(FP8X4), scales=w1_s[e][:], in_=w1_bf[e][:])
 
         def first_layer(e):
             if e in HOLD_H:
@@ -182,42 +192,58 @@ def tile_moe_ogt_gelu_silu_kernel(
             else:
                 h_q[e] = keep.tile([P, C], U32, name="h_q%d" % e, tag=HOLD_Q.get(e, "h_q%d" % e), align_bytes=64)
             h_s[e] = keep.tile([P, C], U8, name="h_s%d" % e, align_bytes=64)
-            nc.vector.quantize_mx(out=h_q[e][:].bitcast(FP8X4), scales=h_s[e][:], in_=h_bf[e][:])
+            parts = 2 if e >= E - FINE else 1
+            for u in range(parts):
+                cols = slice(u * C // parts, (u + 1) * C // parts)
+                nc.vector.quantize_mx(
+                    out=h_q[e][:, cols].bitcast(FP8X4),
+                    scales=h_s[e][:, cols],
+                    in_=h_bf[e][:, u * PACK * C // parts : (u + 1) * PACK * C // parts],
+                )
 
-        def prepare_w2(a):
-            w2_bf = ring.tile([P, 2 * PACK * N], BF16, name="w2_bf", align_bytes=64)
-            copy_on(
-                CAST2[a],
-                w2_bf[:].rearrange("p (e c i j) -> p e c j i", e=2, i=PACK, j=PACK),
-                w2_raw[a][:].rearrange("p e j (c i) -> p e c j i", i=PACK),
-            )
-            w2_q[a] = ring.tile([P, 2 * N], U32, name="w2_q", align_bytes=64)
-            w2_s[a] = ring.tile([P, 2 * N], U8, name="w2_s", align_bytes=64)
-            nc.vector.quantize_mx(out=w2_q[a][:].bitcast(FP8X4), scales=w2_s[a][:], in_=w2_bf[:])
+        def round_w2(a):
+            w2_bf[a] = keep.tile([P, 2 * PACK * N], BF16, name="w2_bf%d" % a, align_bytes=64)
+            dst = w2_bf[a][:].rearrange("p (e c i j) -> p e c j i", e=2, i=PACK, j=PACK)
+            src = w2_raw[a][:].rearrange("p e j (c i) -> p e c j i", i=PACK)
+            if CAST2[a][0] == CAST2[a][1]:
+                copy_on(CAST2[a][0], dst, src)
+            else:
+                for b in range(2):
+                    copy_on(CAST2[a][b], dst[:, b], src[:, b])
+
+        def quantise_w2(a):
+            w2_q[a] = keep.tile([P, 2 * N], U32, name="w2_q%d" % a, align_bytes=64)
+            w2_s[a] = keep.tile([P, 2 * N], U8, name="w2_s%d" % a, align_bytes=64)
+            nc.vector.quantize_mx(out=w2_q[a][:].bitcast(FP8X4), scales=w2_s[a][:], in_=w2_bf[a][:])
 
         def second_layer(e):
             a, b = divmod(e, 2)
-            alone = e >= E - 2 and SPLIT_Y
-            if b == 0 or alone:
-                y_ps[a] = psum.tile([P, 2 * C], F32, name="y_ps")
-            nc.tensor.matmul_mx(
-                out=y_ps[a][:, b * C : (b + 1) * C],
-                lhsT=w2_q[a][:, b * N : (b + 1) * N].bitcast(FP8X4),
-                lhsT_scale=w2_s[a][:, b * N : (b + 1) * N],
-                rhs=h_q[e][:].bitcast(FP8X4),
-                rhs_scale=h_s[e][:],
-                start=True,
-                stop=True,
-            )
-            if alone:
-                copy_on(SPLIT_Y[b], y_sb[:, e * C : (e + 1) * C], y_ps[a][:, b * C : (b + 1) * C])
-            elif b == 1:
-                copy_on(YCOPY[a], y_sb[:, a * 2 * C : (a + 1) * 2 * C], y_ps[a][:])
+            alone = e >= E - 2
+            parts = 2 if e >= E - FINE else 1
+            for u in range(parts):
+                if b == 0 or alone:
+                    y_ps[a] = psum.tile([P, 2 * C], F32, name="y_ps", tag="bank%d" % Y_BANK[e][u], bufs=1)
+                slots = slice(u * C // parts, (u + 1) * C // parts)
+                cols = slice(b * C + slots.start, b * C + slots.stop)
+                nc.tensor.matmul_mx(
+                    out=y_ps[a][:, cols],
+                    lhsT=w2_q[a][:, b * N : (b + 1) * N].bitcast(FP8X4),
+                    lhsT_scale=w2_s[a][:, b * N : (b + 1) * N],
+                    rhs=h_q[e][:, slots].bitcast(FP8X4),
+                    rhs_scale=h_s[e][:, slots],
+                    start=True,
+                    stop=True,
+                )
+                if alone:
+                    copy_on(SPLIT_Y[b], y_sb[:, e * C + slots.start : e * C + slots.stop], y_ps[a][:, cols])
+                elif b == 1:
+                    copy_on(YCOPY[a], y_sb[:, a * 2 * C : (a + 1) * 2 * C], y_ps[a][:])
 
         def output_gate():
+            o_sb = keep.tile([P, T], F32, name="o_sb", tag="h_bf%d" % (E - 1) if SIDE else "o_sb", align_bytes=64)
             for u in range(2):
                 tokens = slice(u * 512, (u + 1) * 512)
-                o_ps = psum.tile([P, 512], F32, name="o_ps", tag="bank%d" % (3 - u), bufs=1)
+                o_ps = psum.tile([P, 512], F32, name="o_ps", tag="bank%d" % (6 + u if SIDE else 3 - u), bufs=1)
                 nc.tensor.matmul_mx(
                     out=o_ps[:],
                     lhsT=wg_w[:].bitcast(FP4X4),
@@ -228,27 +254,40 @@ def tile_moe_ogt_gelu_silu_kernel(
                     stop=True,
                 )
                 nc.scalar.activation(o_sb[:, tokens], o_ps[:], ACT.Silu)
+            return o_sb
 
-        gate_ps = psum.tile([P, P], F32, name="gate_ps", tag="total")
+        def second_pair(a):
+            round_w2(a)
+            for e in (2 * a, 2 * a + 1):
+                if e not in h_q and HOLD_Q.get(e) != "w2_bf%d" % a:
+                    quantise_h(e)
+            quantise_w2(a)
+            for e in (2 * a, 2 * a + 1):
+                if e not in h_q:
+                    quantise_h(e)
+                second_layer(e)
+
+        for g in range(2):
+            gather(g)
+        for e in range(E):
+            round_w1(e)
+            for f in range(E):
+                if HOLD_R.get(f) == e:
+                    quantise_h(f)
+            quantise_w1(e)
+            if e < 2:
+                gather(e + 2)
+            first_layer(e)
+            if e == PAIR0_AFTER:
+                second_pair(0)
+        for a in range(1, E // 2):
+            second_pair(a)
+
+        gate_ps = psum.tile([P, P], F32, name="gate_ps", tag="bank5", bufs=1)
         nc.tensor.transpose(gate_ps[:], gate_rows[:], ident[:])
         nc.scalar.copy(gate_cols[:], gate_ps[:, : 2 * T // P])
 
-        for s in range(E + LAG_Q):
-            if s < E:
-                if s * C % PIECE == 0:
-                    gather(s * C // PIECE)
-                round_w1(s)
-            if 1 <= s <= E:
-                quantise_w1(s - 1)
-            if 0 <= s - LAG_H < E:
-                first_layer(s - LAG_H)
-            if 0 <= s - LAG_Q < E:
-                quantise_h(s - LAG_Q)
-                if (s - LAG_Q) % 2 == 0:
-                    prepare_w2((s - LAG_Q) // 2)
-                second_layer(s - LAG_Q)
-
-        output_gate()
+        o_sb = output_gate()
 
         totals = []
         for c in range(TURNED // CHUNK):
@@ -257,10 +296,7 @@ def tile_moe_ogt_gelu_silu_kernel(
             for r in range(2):
                 picked = ring.tile([P, CHUNK], F32, name="picked", bufs=4)
                 nc.vector.tensor_copy(picked[:], y_sb[:].indirect(pos_sb[r][:, c * CHUNK // 16 : (c + 1) * CHUNK // 16]))
-                if c % 2 == 0:
-                    turned = psum.tile([P, CHUNK], F32, name="turned", tag="bank%d" % r, bufs=1)
-                else:
-                    turned = psum.tile([P, CHUNK], F32, name="turned", tag="y_ps")
+                turned = psum.tile([P, CHUNK], F32, name="turned", tag="bank%d" % ((2 * c + r) % 4), bufs=1)
                 for b in range(CHUNK // P):
                     cols = slice(b * P, (b + 1) * P)
                     nc.tensor.transpose(turned[:, cols], picked[:, cols], ident[:])
@@ -268,7 +304,7 @@ def tile_moe_ogt_gelu_silu_kernel(
                     cols = slice(b * P, (b + 1) * P)
                     g = r * (T // P) + c * (CHUNK // P) + b
                     nc.scalar.activation(scaled[:, r, cols], turned[:, cols], ACT.Copy, scale=gate_cols[:, g : g + 1])
-            total = psum.tile([P, CHUNK], F32, name="total")
+            total = psum.tile([P, CHUNK], F32, name="total", tag="bank%d" % (4 + c), bufs=1)
             for b in range(CHUNK // P):
                 cols = slice(b * P, (b + 1) * P)
                 for r in range(2):
@@ -286,7 +322,7 @@ def tile_moe_ogt_gelu_silu_kernel(
         if not LATE:
             for c in range(TURNED // CHUNK):
                 finish_turned(c)
-        for t0, t1 in zip(CUTS[:-1], CUTS[1:]):
+        for t0, t1 in zip(CUTS[TURNED][:-1], CUTS[TURNED][1:]):
             parts = []
             for r in range(2):
                 part = keep.tile([P, t1 - t0], F32, name="part%d_%d" % (t0, r))

@@ -26,22 +26,22 @@ HALF_Q = 1
 FINE = 1
 SIDE = 1
 Y_BANK = {0: (4,), 2: (5,), 4: (0,), 6: (1,), 7: (4, 2)}
-PAIR0_AFTER = 3
+PAIR0_AFTER = 5
 RAW = PACK * H * 4
 HOLD_X = {2: "w1_bf0", 3: "w1_bf1"}
 CAST = ("SS","SS","SS","VV","SS","VV","VV","VS")
-CAST2 = ("VV","VV","SV","VV")
+CAST2 = ("SS","VV","SV","VV")
 YCOPY = "SSSV"
-HOLD_H = {0: 1, 1: 2, 2: 4, 3: 4, 5: 6, 6: 7}
+HOLD_H = {0: 1, 1: 2, 2: 4, 3: 4, 6: 7}
 HOLD_Q = {7: "w2_bf3"}
 CHUNK = 256
 LATE = 1
 TURNED = 512
 WHOLE = 1
-CUTS = {512: (512, 768, 1024), 768: (768, 1024), 256: (256, 512, 768, 1024)}
-HOLD_W = {2: 3}
+CUTS = {512: (512, 768, 1024)}
+HOLD_W = {2: 3, 4: 5}
 SPLIT_Y = "SV"
-LOADS = "a0 a1 x a2 a3 a4 b0 a5 a6 a7 b1 b2 b3 wg s0 s1 s2 s3 g p0 p1 h0 h1"
+LOADS = "a0 a1 x a2 a3 a4 a5 b0 a6 a7 b1 b2 b3 wg s0 s1 s2 s3 g p0 p1 h0 h1"
 
 
 def tile_moe_ogt_gelu_silu_kernel(
@@ -128,9 +128,11 @@ def tile_moe_ogt_gelu_silu_kernel(
             xg_s[g] = keep.tile([P, PIECE], U8, name="xg_s%d" % g, align_bytes=64)
             piece = offs_sb[:, g * PIECE // 16 : (g + 1) * PIECE // 16]
             nc.vector.tensor_copy(xg_s[g][:], x_s[:].indirect(piece))
-            for u in range(2):
+            width = C if g == 0 else PIECE
+            for first in range(0, PIECE, width):
                 nc.vector.tensor_copy(
-                    xg_w[g][:, u * C : (u + 1) * C], x_w[:].bitcast(U32).indirect(piece[:, u * C // 16 : (u + 1) * C // 16])
+                    xg_w[g][:, first : first + width],
+                    x_w[:].bitcast(U32).indirect(piece[:, first // 16 : (first + width) // 16]),
                 )
 
         def round_w1(e):
@@ -212,7 +214,10 @@ def tile_moe_ogt_gelu_silu_kernel(
                     copy_on(CAST2[a][b], dst[:, b], src[:, b])
 
         def quantise_w2(a):
-            w2_q[a] = keep.tile([P, 2 * N], U32, name="w2_q%d" % a, align_bytes=64)
+            if a == 0:
+                w2_q[a] = reuse.tile([P, 2 * N], U32, name="w2_q0", align_bytes=64, offset=6 * RAW + 4096)
+            else:
+                w2_q[a] = keep.tile([P, 2 * N], U32, name="w2_q%d" % a, align_bytes=64)
             w2_s[a] = keep.tile([P, 2 * N], U8, name="w2_s%d" % a, align_bytes=64)
             nc.vector.quantize_mx(out=w2_q[a][:].bitcast(FP8X4), scales=w2_s[a][:], in_=w2_bf[a][:])
 
@@ -257,7 +262,8 @@ def tile_moe_ogt_gelu_silu_kernel(
             return o_sb
 
         def second_pair(a):
-            round_w2(a)
+            if a not in w2_bf:
+                round_w2(a)
             for e in (2 * a, 2 * a + 1):
                 if e not in h_q and HOLD_Q.get(e) != "w2_bf%d" % a:
                     quantise_h(e)

@@ -20,28 +20,35 @@ ALU = mybir.AluOpType
 
 P = 128
 PACK = 4
-PIECE = 512
-HOLD_R = {2: 5, 3: 6, 4: 6, 5: 7}
-HALF_Q = 1
-FINE = 1
-SIDE = 1
-Y_BANK = {0: (4,), 2: (5,), 4: (0,), 6: (1,), 7: (4, 2)}
-PAIR0_AFTER = 5
-RAW = PACK * H * 4
-HOLD_X = {2: "w1_bf0", 3: "w1_bf1"}
-CAST = ("SS","SS","SS","VV","SS","VV","VV","VS")
-CAST2 = ("SS","VV","SV","VV")
-YCOPY = "SSSV"
-HOLD_H = {0: 1, 1: 2, 2: 4, 3: 4, 6: 7}
-HOLD_Q = {7: "w2_bf3"}
-CHUNK = 256
-LATE = 1
+PAIR = 2 * C
+LAST = E - 1
+BANK = 512
+
+GATHER_PHASE = 3
+RELIEF = 4
+WORDS_AFTER = 2
+FIRST_W2_BEFORE = 6
+H_LAG = 2
 TURNED = 512
-WHOLE = 1
-CUTS = {512: (512, 768, 1024)}
-HOLD_W = {2: 3, 4: 5}
-SPLIT_Y = "SV"
-LOADS = "a0 a1 x a2 a3 a4 a5 b0 a6 a7 b1 b2 b3 wg s0 s1 s2 s3 g p0 p1 h0 h1"
+CHUNK = 256
+
+RAW = PACK * H * 4
+AT_H_BF = 0
+AT_CODES = RAW // 2
+AT_H_Q = 3 * RAW // 4
+
+
+def scalar_rounds(e):
+    return e < GATHER_PHASE or e == RELIEF or e == LAST
+
+
+def vector_rounds(e):
+    return not scalar_rounds(e) or e == LAST
+
+
+def h_waits_for(e):
+    later = [f for f in range(e + H_LAG, E) if vector_rounds(f)]
+    return later[0] if later else None
 
 
 def tile_moe_ogt_gelu_silu_kernel(
@@ -52,7 +59,7 @@ def tile_moe_ogt_gelu_silu_kernel(
         keep = ctx.enter_context(tc.tile_pool(name="keep", bufs=1))
         reuse = ctx.enter_context(tc.tile_pool(name="reuse", bufs=1))
         ring = ctx.enter_context(tc.tile_pool(name="ring", bufs=2))
-        psum = ctx.enter_context(tc.psum_pool(name="psum", bufs=2))
+        psum = ctx.enter_context(tc.psum_pool(name="psum", bufs=1))
 
         offs_sb = keep.tile([P, SLOTS // 16], U16, name="offs_sb")
         pos_sb = [keep.tile([P, T // 16], U16, name="pos%d_sb" % r) for r in range(2)]
@@ -60,7 +67,9 @@ def tile_moe_ogt_gelu_silu_kernel(
         x_s = keep.tile([P, T], U8, name="x_s", align_bytes=64)
         wg_w = keep.tile([P, 2 * N], U8, name="wg_w", align_bytes=64)
         wg_s = keep.tile([P, N], U8, name="wg_s", align_bytes=64)
-        w1_raw = [reuse.tile([P, PACK, H], F32, name="w1_raw%d" % e, align_bytes=64, offset=e * RAW) for e in range(E)]
+        w1_raw = [
+            reuse.tile([P, PACK, H], F32, name="w1_raw%d" % e, align_bytes=64, offset=e * RAW) for e in range(E)
+        ]
         w2_raw = [keep.tile([P, 2, PACK, N], F32, name="w2_raw%d" % a, align_bytes=64) for a in range(E // 2)]
         gate_rows = keep.tile([P, P], F32, name="gate_rows")
         gate_cols = keep.tile([P, 2 * T // P], F32, name="gate_cols")
@@ -75,29 +84,12 @@ def tile_moe_ogt_gelu_silu_kernel(
         nc.vector.memset(warm[:], 0.0)
         nc.vector.memset(gate_rows[:], 0.0)
 
-        side = nc.sync
+        def bank(shape, name, number):
+            return psum.tile(shape, F32, name=name, tag="bank%d" % number)
 
-        def load_scale_rows(queue, plane, rows, r):
-            queue.dma_start(plane[:].bitcast(I32)[r:P:32, :], rows[0].bitcast(I32)[r:16:4, :])
+        def behind_rounding(e, at, shape, dtype, name):
+            return reuse.tile(shape, dtype, name=name, align_bytes=64, offset=e * RAW + at)
 
-        def load_w1(e):
-            nc.sync.dma_start(w1_raw[e][:], w1[e].rearrange("(p j) c -> p j c", j=PACK))
-
-        def load_w2(a):
-            nc.sync.dma_start(
-                w2_raw[a][:].rearrange("p e j n -> p e (j n)"),
-                w2[2 * a : 2 * a + 2].rearrange("e (p j) n -> p e (j n)", j=PACK),
-            )
-
-        loads = {
-            "x": lambda: nc.sync.dma_start(x_w[:], x_words[0].rearrange("p t d -> p (t d)").bitcast(I32)),
-            "wg": lambda: side.dma_start(wg_w[:].bitcast(I32), wg_words[0].bitcast(I32)),
-            "p0": lambda: nc.sync.dma_start(pos_sb[0][:], pos1),
-            "p1": lambda: nc.sync.dma_start(pos_sb[1][:], pos2),
-            "h0": lambda: nc.sync.dma_start(gate_sb[0][:], gate[0][:, TURNED:]),
-            "h1": lambda: nc.sync.dma_start(gate_sb[1][:], gate[1][:, TURNED:]),
-            "g": lambda: side.dma_start(gate_rows[0:16, :], gate[:, 0, :].rearrange("r (c q) -> r c q", q=P)),
-        }
         nc.sync.dma_start(offs_sb[:], offs)
         for q in range(4):
             nc.sync.dma_start(
@@ -105,80 +97,93 @@ def tile_moe_ogt_gelu_silu_kernel(
                 x_scales[0].bitcast(I32)[4 * q : 4 * q + 4, :].partition_broadcast(8),
             )
         nc.scalar.activation(warm_out[:], warm[:], ACT.Gelu_apprx_tanh)
-        for what in LOADS.split():
-            if what in loads:
-                loads[what]()
-            elif what[0] == "s":
-                load_scale_rows(side, wg_s, wg_scales, int(what[1]))
-            elif what[0] == "a":
-                load_w1(int(what[1]))
-            else:
-                load_w2(int(what[1]))
 
-        def copy_on(engine, dst, src):
-            if engine == "V":
-                nc.vector.tensor_copy(dst, src)
-            else:
-                nc.scalar.copy(dst, src)
+        def load_w2(a):
+            nc.sync.dma_start(
+                w2_raw[a][:].rearrange("p e j n -> p e (j n)"),
+                w2[2 * a : 2 * a + 2].rearrange("e (p j) n -> p e (j n)", j=PACK),
+            )
 
-        w1_bf, w1_q, w1_s, xg_w, xg_s, h_bf, h_q, h_s, w2_bf, w2_q, w2_s, y_ps = ({} for i in range(12))
+        for e in range(E):
+            if e == WORDS_AFTER:
+                nc.sync.dma_start(x_w[:], x_words[0].rearrange("p t d -> p (t d)").bitcast(I32))
+            if e == FIRST_W2_BEFORE:
+                load_w2(0)
+            nc.sync.dma_start(w1_raw[e][:], w1[e].rearrange("(p j) c -> p j c", j=PACK))
+        for a in range(1, E // 2):
+            load_w2(a)
+        nc.sync.dma_start(wg_w[:].bitcast(I32), wg_words[0].bitcast(I32))
+        for r in range(4):
+            nc.sync.dma_start(wg_s[:].bitcast(I32)[r:P:32, :], wg_scales[0].bitcast(I32)[r:16:4, :])
+        nc.sync.dma_start(gate_rows[0:16, :], gate[:, 0, :].rearrange("r (c q) -> r c q", q=P))
+        nc.sync.dma_start(pos_sb[0][:], pos1)
+        nc.sync.dma_start(pos_sb[1][:], pos2)
+        for r in range(2):
+            nc.sync.dma_start(gate_sb[r][:], gate[r][:, TURNED:])
 
-        def gather(g):
-            xg_w[g] = keep.tile([P, PIECE], U32, name="xg_w%d" % g, tag=HOLD_X.get(g, "xg_w%d" % g), align_bytes=64)
-            xg_s[g] = keep.tile([P, PIECE], U8, name="xg_s%d" % g, align_bytes=64)
-            piece = offs_sb[:, g * PIECE // 16 : (g + 1) * PIECE // 16]
-            nc.vector.tensor_copy(xg_s[g][:], x_s[:].indirect(piece))
-            width = C if g == 0 else PIECE
-            for first in range(0, PIECE, width):
+        w1_bf, w1_q, w1_s, xg_w, xg_s, h_bf, h_q, h_s, w2_bf, w2_q, w2_s = ({} for i in range(11))
+
+        def gather_tokens(a):
+            tag = "w1_bf%d" % (a - 2) if a >= 2 else "xg_w%d" % a
+            xg_w[a] = keep.tile([P, PAIR], U32, name="xg_w%d" % a, tag=tag, align_bytes=64)
+            xg_s[a] = keep.tile([P, PAIR], U8, name="xg_s%d" % a, align_bytes=64)
+            entries = offs_sb[:, a * PAIR // 16 : (a + 1) * PAIR // 16]
+            nc.vector.tensor_copy(xg_s[a][:], x_s[:].indirect(entries))
+            width = C if a == 0 else PAIR
+            for first in range(0, PAIR, width):
                 nc.vector.tensor_copy(
-                    xg_w[g][:, first : first + width],
-                    x_w[:].bitcast(U32).indirect(piece[:, first // 16 : (first + width) // 16]),
+                    xg_w[a][:, first : first + width],
+                    x_w[:].bitcast(U32).indirect(entries[:, first // 16 : (first + width) // 16]),
                 )
 
         def round_w1(e):
             w1_bf[e] = keep.tile([P, PACK * H], BF16, name="w1_bf%d" % e, align_bytes=64)
             dst = w1_bf[e][:].rearrange("p (t m j) -> p m j t", t=PACK, j=PACK)
             src = w1_raw[e][:].rearrange("p j (m t) -> p m j t", t=PACK)
-            if CAST[e][0] == CAST[e][1] and WHOLE:
-                copy_on(CAST[e][0], dst, src)
+            if e == LAST:
+                nc.vector.tensor_copy(dst[:, :, :, 0:2], src[:, :, :, 0:2])
+                nc.scalar.copy(dst[:, :, :, 2:4], src[:, :, :, 2:4])
+            elif scalar_rounds(e):
+                nc.scalar.copy(dst, src)
             else:
-                copy_on(CAST[e][0], dst[:, :, :, 0:2], src[:, :, :, 0:2])
-                copy_on(CAST[e][1], dst[:, :, :, 2:4], src[:, :, :, 2:4])
+                nc.vector.tensor_copy(dst, src)
+
+        def quantised_with(e):
+            return e + 1 if e < LAST and not vector_rounds(e) and not scalar_rounds(e + 1) else e
 
         def quantise_w1(e):
-            if e in HOLD_W:
-                w1_q[e] = reuse.tile([P, H], U32, name="w1_q%d" % e, align_bytes=64, offset=HOLD_W[e] * RAW + 4096)
+            if quantised_with(e) != e:
+                w1_q[e] = behind_rounding(e + 1, AT_CODES, [P, H], U32, "w1_q%d" % e)
             else:
                 w1_q[e] = keep.tile([P, H], U32, name="w1_q%d" % e, align_bytes=64)
             w1_s[e] = keep.tile([P, H], U8, name="w1_s%d" % e, align_bytes=64)
-            if CAST[e] == "VS" and HALF_Q:
-                for u in range(2):
-                    cols = slice(u * H // 2, (u + 1) * H // 2)
-                    nc.vector.quantize_mx(
-                        out=w1_q[e][:, cols].bitcast(FP8X4), scales=w1_s[e][:, cols], in_=w1_bf[e][:, u * 2 * H : (u + 1) * 2 * H]
-                    )
-            else:
-                nc.vector.quantize_mx(out=w1_q[e][:].bitcast(FP8X4), scales=w1_s[e][:], in_=w1_bf[e][:])
+            width = H // 2 if e == LAST else H
+            for first in range(0, H, width):
+                cols = slice(first, first + width)
+                nc.vector.quantize_mx(
+                    out=w1_q[e][:, cols].bitcast(FP8X4),
+                    scales=w1_s[e][:, cols],
+                    in_=w1_bf[e][:, PACK * first : PACK * (first + width)],
+                )
 
         def first_layer(e):
-            if e in HOLD_H:
-                h_bf[e] = reuse.tile(
-                    [P, PACK * C], BF16, name="h_bf%d" % e, align_bytes=64, offset=HOLD_H[e] * RAW + e % 2 * 2048
-                )
+            after = quantised_with(e) + 1
+            if after < E and scalar_rounds(after):
+                h_bf[e] = behind_rounding(after, AT_H_BF + e % 2 * 2 * PACK * C, [P, PACK * C], BF16, "h_bf%d" % e)
             else:
                 h_bf[e] = keep.tile([P, PACK * C], BF16, name="h_bf%d" % e, align_bytes=64)
-            g, first = divmod(e * C, PIECE)
-            for u in range(2):
+            a, first = divmod(e * C, PAIR)
+            for u in range(C // P):
                 slots = slice(first + u * P, first + (u + 1) * P)
-                h_ps = psum.tile([P, PACK, P], F32, name="h_ps", tag="bank%d" % ((2 * e + u) % 4), bufs=1)
+                h_ps = bank([P, PACK, P], "h_ps", (2 * e + u) % 4)
                 for t in range(PACK):
                     cols = slice(t * P, (t + 1) * P)
                     nc.tensor.matmul_mx(
                         out=h_ps[:, t, :],
                         lhsT=w1_q[e][:, cols].bitcast(FP8X4),
                         lhsT_scale=w1_s[e][:, cols],
-                        rhs=xg_w[g][:, slots].bitcast(FP8X4),
-                        rhs_scale=xg_s[g][:, slots],
+                        rhs=xg_w[a][:, slots].bitcast(FP8X4),
+                        rhs_scale=xg_s[a][:, slots],
                         start=True,
                         stop=True,
                     )
@@ -189,120 +194,115 @@ def tile_moe_ogt_gelu_silu_kernel(
                 )
 
         def quantise_h(e):
-            if e in HOLD_R:
-                h_q[e] = reuse.tile([P, C], U32, name="h_q%d" % e, align_bytes=64, offset=HOLD_R[e] * RAW + 6144 + e % 2 * 1024)
+            if h_waits_for(e) is not None:
+                h_q[e] = behind_rounding(h_waits_for(e), AT_H_Q + e % 2 * 4 * C, [P, C], U32, "h_q%d" % e)
             else:
-                h_q[e] = keep.tile([P, C], U32, name="h_q%d" % e, tag=HOLD_Q.get(e, "h_q%d" % e), align_bytes=64)
+                tag = "w2_bf%d" % (e // 2) if e == LAST else "h_q%d" % e
+                h_q[e] = keep.tile([P, C], U32, name="h_q%d" % e, tag=tag, align_bytes=64)
             h_s[e] = keep.tile([P, C], U8, name="h_s%d" % e, align_bytes=64)
-            parts = 2 if e >= E - FINE else 1
-            for u in range(parts):
-                cols = slice(u * C // parts, (u + 1) * C // parts)
+            width = P if e == LAST else C
+            for first in range(0, C, width):
+                cols = slice(first, first + width)
                 nc.vector.quantize_mx(
                     out=h_q[e][:, cols].bitcast(FP8X4),
                     scales=h_s[e][:, cols],
-                    in_=h_bf[e][:, u * PACK * C // parts : (u + 1) * PACK * C // parts],
+                    in_=h_bf[e][:, PACK * first : PACK * (first + width)],
                 )
 
         def round_w2(a):
             w2_bf[a] = keep.tile([P, 2 * PACK * N], BF16, name="w2_bf%d" % a, align_bytes=64)
             dst = w2_bf[a][:].rearrange("p (e c i j) -> p e c j i", e=2, i=PACK, j=PACK)
             src = w2_raw[a][:].rearrange("p e j (c i) -> p e c j i", i=PACK)
-            if CAST2[a][0] == CAST2[a][1]:
-                copy_on(CAST2[a][0], dst, src)
+            if a % 2 == 0:
+                nc.scalar.copy(dst, src)
             else:
-                for b in range(2):
-                    copy_on(CAST2[a][b], dst[:, b], src[:, b])
+                nc.vector.tensor_copy(dst, src)
 
         def quantise_w2(a):
             if a == 0:
-                w2_q[a] = reuse.tile([P, 2 * N], U32, name="w2_q0", align_bytes=64, offset=6 * RAW + 4096)
+                w2_q[a] = behind_rounding(LAST, AT_CODES, [P, 2 * N], U32, "w2_q0")
             else:
                 w2_q[a] = keep.tile([P, 2 * N], U32, name="w2_q%d" % a, align_bytes=64)
             w2_s[a] = keep.tile([P, 2 * N], U8, name="w2_s%d" % a, align_bytes=64)
             nc.vector.quantize_mx(out=w2_q[a][:].bitcast(FP8X4), scales=w2_s[a][:], in_=w2_bf[a][:])
 
-        def second_layer(e):
+        def second_product(y_ps, e, first, width):
             a, b = divmod(e, 2)
-            alone = e >= E - 2
-            parts = 2 if e >= E - FINE else 1
-            for u in range(parts):
-                if b == 0 or alone:
-                    y_ps[a] = psum.tile([P, 2 * C], F32, name="y_ps", tag="bank%d" % Y_BANK[e][u], bufs=1)
-                slots = slice(u * C // parts, (u + 1) * C // parts)
-                cols = slice(b * C + slots.start, b * C + slots.stop)
-                nc.tensor.matmul_mx(
-                    out=y_ps[a][:, cols],
-                    lhsT=w2_q[a][:, b * N : (b + 1) * N].bitcast(FP8X4),
-                    lhsT_scale=w2_s[a][:, b * N : (b + 1) * N],
-                    rhs=h_q[e][:, slots].bitcast(FP8X4),
-                    rhs_scale=h_s[e][:, slots],
-                    start=True,
-                    stop=True,
-                )
-                if alone:
-                    copy_on(SPLIT_Y[b], y_sb[:, e * C + slots.start : e * C + slots.stop], y_ps[a][:, cols])
-                elif b == 1:
-                    copy_on(YCOPY[a], y_sb[:, a * 2 * C : (a + 1) * 2 * C], y_ps[a][:])
+            nc.tensor.matmul_mx(
+                out=y_ps,
+                lhsT=w2_q[a][:, b * N : (b + 1) * N].bitcast(FP8X4),
+                lhsT_scale=w2_s[a][:, b * N : (b + 1) * N],
+                rhs=h_q[e][:, first : first + width].bitcast(FP8X4),
+                rhs_scale=h_s[e][:, first : first + width],
+                start=True,
+                stop=True,
+            )
 
-        def output_gate():
-            o_sb = keep.tile([P, T], F32, name="o_sb", tag="h_bf%d" % (E - 1) if SIDE else "o_sb", align_bytes=64)
-            for u in range(2):
-                tokens = slice(u * 512, (u + 1) * 512)
-                o_ps = psum.tile([P, 512], F32, name="o_ps", tag="bank%d" % (6 + u if SIDE else 3 - u), bufs=1)
-                nc.tensor.matmul_mx(
-                    out=o_ps[:],
-                    lhsT=wg_w[:].bitcast(FP4X4),
-                    lhsT_scale=wg_s[:],
-                    rhs=x_w[:, tokens].bitcast(FP8X4),
-                    rhs_scale=x_s[:, tokens],
-                    start=True,
-                    stop=True,
-                )
-                nc.scalar.activation(o_sb[:, tokens], o_ps[:], ACT.Silu)
-            return o_sb
-
-        def second_pair(a):
-            if a not in w2_bf:
-                round_w2(a)
+        def second_layer(a):
+            round_w2(a)
             for e in (2 * a, 2 * a + 1):
-                if e not in h_q and HOLD_Q.get(e) != "w2_bf%d" % a:
+                if e not in h_q and e != LAST:
                     quantise_h(e)
             quantise_w2(a)
-            for e in (2 * a, 2 * a + 1):
-                if e not in h_q:
-                    quantise_h(e)
-                second_layer(e)
+            if 2 * a + 1 < LAST:
+                y_ps = bank([P, PAIR], "y_ps", (4, 5, 0)[a])
+                for b in range(2):
+                    second_product(y_ps[:, b * C : (b + 1) * C], 2 * a + b, 0, C)
+                nc.scalar.copy(y_sb[:, a * PAIR : (a + 1) * PAIR], y_ps[:])
+            else:
+                y_ps = bank([P, PAIR], "y_ps", 1)
+                second_product(y_ps[:, 0:C], LAST - 1, 0, C)
+                nc.vector.tensor_copy(y_sb[:, (LAST - 1) * C : LAST * C], y_ps[:, 0:C])
+                quantise_h(LAST)
+                for first, number in ((0, 4), (P, 2)):
+                    y_ps = bank([P, PAIR], "y_ps", number)
+                    cols = slice(C + first, C + first + P)
+                    second_product(y_ps[:, cols], LAST, first, P)
+                    nc.vector.tensor_copy(y_sb[:, LAST * C + first : LAST * C + first + P], y_ps[:, cols])
 
-        for g in range(2):
-            gather(g)
+        for a in range(2):
+            gather_tokens(a)
         for e in range(E):
             round_w1(e)
-            for f in range(E):
-                if HOLD_R.get(f) == e:
-                    quantise_h(f)
             quantise_w1(e)
+            for f in range(e):
+                if h_waits_for(f) == e:
+                    quantise_h(f)
             if e < 2:
-                gather(e + 2)
+                gather_tokens(e + 2)
             first_layer(e)
-            if e == PAIR0_AFTER:
-                second_pair(0)
+            if e == FIRST_W2_BEFORE - 1:
+                second_layer(0)
         for a in range(1, E // 2):
-            second_pair(a)
+            second_layer(a)
 
-        gate_ps = psum.tile([P, P], F32, name="gate_ps", tag="bank5", bufs=1)
+        gate_ps = bank([P, P], "gate_ps", 5)
         nc.tensor.transpose(gate_ps[:], gate_rows[:], ident[:])
         nc.scalar.copy(gate_cols[:], gate_ps[:, : 2 * T // P])
 
-        o_sb = output_gate()
+        o_sb = keep.tile([P, T], F32, name="o_sb", tag="h_bf%d" % LAST, align_bytes=64)
+        for u in range(T // BANK):
+            tokens = slice(u * BANK, (u + 1) * BANK)
+            o_ps = bank([P, BANK], "o_ps", 6 + u)
+            nc.tensor.matmul_mx(
+                out=o_ps[:],
+                lhsT=wg_w[:].bitcast(FP4X4),
+                lhsT_scale=wg_s[:],
+                rhs=x_w[:, tokens].bitcast(FP8X4),
+                rhs_scale=x_s[:, tokens],
+                start=True,
+                stop=True,
+            )
+            nc.scalar.activation(o_sb[:, tokens], o_ps[:], ACT.Silu)
 
         totals = []
         for c in range(TURNED // CHUNK):
-            tokens = slice(c * CHUNK, (c + 1) * CHUNK)
             scaled = ring.tile([P, 2, CHUNK], F32, name="scaled")
             for r in range(2):
-                picked = ring.tile([P, CHUNK], F32, name="picked", bufs=4)
-                nc.vector.tensor_copy(picked[:], y_sb[:].indirect(pos_sb[r][:, c * CHUNK // 16 : (c + 1) * CHUNK // 16]))
-                turned = psum.tile([P, CHUNK], F32, name="turned", tag="bank%d" % ((2 * c + r) % 4), bufs=1)
+                picked = ring.tile([P, CHUNK], F32, name="picked", bufs=2 * TURNED // CHUNK)
+                entries = pos_sb[r][:, c * CHUNK // 16 : (c + 1) * CHUNK // 16]
+                nc.vector.tensor_copy(picked[:], y_sb[:].indirect(entries))
+                turned = bank([P, CHUNK], "turned", 2 * c + r)
                 for b in range(CHUNK // P):
                     cols = slice(b * P, (b + 1) * P)
                     nc.tensor.transpose(turned[:, cols], picked[:, cols], ident[:])
@@ -310,7 +310,7 @@ def tile_moe_ogt_gelu_silu_kernel(
                     cols = slice(b * P, (b + 1) * P)
                     g = r * (T // P) + c * (CHUNK // P) + b
                     nc.scalar.activation(scaled[:, r, cols], turned[:, cols], ACT.Copy, scale=gate_cols[:, g : g + 1])
-            total = psum.tile([P, CHUNK], F32, name="total", tag="bank%d" % (4 + c), bufs=1)
+            total = bank([P, CHUNK], "total", 4 + c)
             for b in range(CHUNK // P):
                 cols = slice(b * P, (b + 1) * P)
                 for r in range(2):
@@ -319,19 +319,11 @@ def tile_moe_ogt_gelu_silu_kernel(
                     )
             totals.append(total)
 
-        def finish_turned(c):
-            tokens = slice(c * CHUNK, (c + 1) * CHUNK)
-            result = keep.tile([P, CHUNK], F32, name="result%d" % c)
-            nc.vector.tensor_tensor(result[:], totals[c][:], o_sb[:, tokens], ALU.mult)
-            nc.sync.dma_start(out[:, tokens], result[:])
-
-        if not LATE:
-            for c in range(TURNED // CHUNK):
-                finish_turned(c)
-        for t0, t1 in zip(CUTS[TURNED][:-1], CUTS[TURNED][1:]):
+        for t0 in range(TURNED, T, CHUNK):
+            t1 = t0 + CHUNK
             parts = []
             for r in range(2):
-                part = keep.tile([P, t1 - t0], F32, name="part%d_%d" % (t0, r))
+                part = keep.tile([P, CHUNK], F32, name="part%d_%d" % (t0, r))
                 nc.vector.tensor_tensor(
                     part[:],
                     y_sb[:].indirect(pos_sb[r][:, t0 // 16 : t1 // 16]),
@@ -339,11 +331,14 @@ def tile_moe_ogt_gelu_silu_kernel(
                     ALU.mult,
                 )
                 parts.append(part)
-            both = keep.tile([P, t1 - t0], F32, name="both%d" % t0)
+            both = keep.tile([P, CHUNK], F32, name="both%d" % t0)
             nc.vector.tensor_tensor(both[:], parts[0][:], parts[1][:], ALU.add)
-            gated = keep.tile([P, t1 - t0], F32, name="gated%d" % t0)
+            gated = keep.tile([P, CHUNK], F32, name="gated%d" % t0)
             nc.vector.tensor_tensor(gated[:], both[:], o_sb[:, t0:t1], ALU.mult)
             nc.sync.dma_start(out[:, t0:t1], gated[:])
-        if LATE:
-            for c in range(TURNED // CHUNK):
-                finish_turned(c)
+
+        for c in range(TURNED // CHUNK):
+            tokens = slice(c * CHUNK, (c + 1) * CHUNK)
+            result = keep.tile([P, CHUNK], F32, name="result%d" % c)
+            nc.vector.tensor_tensor(result[:], totals[c][:], o_sb[:, tokens], ALU.mult)
+            nc.sync.dma_start(out[:, tokens], result[:])

@@ -92,7 +92,8 @@ def tile_moe_ogt_gelu_silu_kernel(
 
         nc.sync.dma_start(offs_sb[:], offs)
         for q in range(4):
-            nc.sync.dma_start(
+            queue = nc.sync if q < 2 else nc.scalar
+            queue.dma_start(
                 x_s[:].bitcast(I32)[32 * q : 32 * q + 32, :],
                 x_scales[0].bitcast(I32)[4 * q : 4 * q + 4, :].partition_broadcast(8),
             )

@@ -24,31 +24,31 @@ PAIR = 2 * C
 LAST = E - 1
 BANK = 512
 
-GATHER_PHASE = 3
-RELIEF = 4
+ROUND1 = "SSSVSVVH"
+ROUND2 = "VVSV"
+POOL_M = 56
 WORDS_AFTER = 2
-FIRST_W2_BEFORE = 6
-H_LAG = 2
+W2_BEFORE = {6: 0}
+GELU_GATE = {1: 2, 2: 4, 3: 4, 6: 7}
+QH_GATE = {2: 5, 3: 6, 4: 7, 5: 7}
+QH_TAG = {}
+QH_TEXT = {0: 3, 1: 3, 2: 5, 3: 6, 4: 7, 5: 7}
+W_GATE = {4: 1, 6: 1}
+Q1_GATE = {4: 5}
+Y_ENG = "SSSV"
+BF_CHAIN = ()
+Q2_GATE = {0: 7}
+W_BF = {}
+W_TEXT = {2: 0, 4: 1, 6: 1}
+W2_TEXT = {0: 5}
 TURNED = 512
 CHUNK = 256
 
 RAW = PACK * H * 4
-AT_H_BF = 0
-AT_CODES = RAW // 2
-AT_H_Q = 3 * RAW // 4
-
-
-def scalar_rounds(e):
-    return e < GATHER_PHASE or e == RELIEF or e == LAST
-
-
-def vector_rounds(e):
-    return not scalar_rounds(e) or e == LAST
-
-
-def h_waits_for(e):
-    later = [f for f in range(e + H_LAG, E) if vector_rounds(f)]
-    return later[0] if later else None
+AT_WORDS = 0
+AT_H_Q = RAW // 2
+AT_ROUNDED = E * RAW
+ROUNDED_STEP = 2560
 
 
 def tile_moe_ogt_gelu_silu_kernel(
@@ -108,11 +108,12 @@ def tile_moe_ogt_gelu_silu_kernel(
         for e in range(E):
             if e == WORDS_AFTER:
                 nc.sync.dma_start(x_w[:], x_words[0].rearrange("p t d -> p (t d)").bitcast(I32))
-            if e == FIRST_W2_BEFORE:
-                load_w2(0)
+            if e in W2_BEFORE:
+                load_w2(W2_BEFORE[e])
             nc.sync.dma_start(w1_raw[e][:], w1[e].rearrange("(p j) c -> p j c", j=PACK))
-        for a in range(1, E // 2):
-            load_w2(a)
+        for a in range(E // 2):
+            if a not in W2_BEFORE.values():
+                load_w2(a)
         nc.sync.dma_start(wg_w[:].bitcast(I32), wg_words[0].bitcast(I32))
         for r in range(4):
             nc.sync.dma_start(wg_s[:].bitcast(I32)[r:P:32, :], wg_scales[0].bitcast(I32)[r:16:4, :])
@@ -122,43 +123,60 @@ def tile_moe_ogt_gelu_silu_kernel(
         for r in range(2):
             nc.sync.dma_start(gate_sb[r][:], gate[r][:, TURNED:])
 
-        w1_bf, w1_q, w1_s, xg_w, xg_s, h_bf, h_q, h_s, w2_bf, w2_q, w2_s = ({} for i in range(11))
+        w1_bf, w1_q, w1_s, xg_w, xg_s, h_bf, h_q, h_s, w2_bf, w2_q, w2_s, h_ps = ({} for i in range(12))
 
-        def gather_tokens(a):
-            tag = "w1_bf%d" % (a - 2) if a >= 2 else "xg_w%d" % a
-            xg_w[a] = keep.tile([P, PAIR], U32, name="xg_w%d" % a, tag=tag, align_bytes=64)
+        def behind_quantise(e, shape, dtype, name):
+            return reuse.tile(shape, dtype, name=name, align_bytes=64, offset=AT_ROUNDED + e * ROUNDED_STEP)
+
+        def gather_scales(a):
             xg_s[a] = keep.tile([P, PAIR], U8, name="xg_s%d" % a, align_bytes=64)
-            entries = offs_sb[:, a * PAIR // 16 : (a + 1) * PAIR // 16]
-            nc.vector.tensor_copy(xg_s[a][:], x_s[:].indirect(entries))
-            width = C if a == 0 else PAIR
-            for first in range(0, PAIR, width):
-                nc.vector.tensor_copy(
-                    xg_w[a][:, first : first + width],
-                    x_w[:].bitcast(U32).indirect(entries[:, first // 16 : (first + width) // 16]),
-                )
+            nc.vector.tensor_copy(xg_s[a][:], x_s[:].indirect(offs_sb[:, a * PAIR // 16 : (a + 1) * PAIR // 16]))
+
+        def gather_words(first, count):
+            if first in W_BF:
+                words = behind_quantise(W_BF[first], [P, count * C], U32, "xg_w%d" % first)
+            elif first in W_GATE:
+                words = behind_rounding(W_GATE[first], AT_WORDS + first // 2 % 2 * 8 * C, [P, count * C], U32, "xg_w%d" % first)
+            else:
+                words = keep.tile([P, count * C], U32, name="xg_w%d" % first, align_bytes=64)
+            entries = offs_sb[:, first * C // 16 : (first + count) * C // 16]
+            nc.vector.tensor_copy(words[:], x_w[:].bitcast(U32).indirect(entries))
+            for b in range(count):
+                xg_w[first + b] = words[:, b * C : (b + 1) * C]
 
         def round_w1(e):
-            w1_bf[e] = keep.tile([P, PACK * H], BF16, name="w1_bf%d" % e, align_bytes=64)
+            if e in BF_CHAIN:
+                w1_bf[e] = behind_quantise(e, [P, PACK * H], BF16, "w1_bf%d" % e)
+            else:
+                w1_bf[e] = keep.tile([P, PACK * H], BF16, name="w1_bf%d" % e, align_bytes=64)
             dst = w1_bf[e][:].rearrange("p (t m j) -> p m j t", t=PACK, j=PACK)
             src = w1_raw[e][:].rearrange("p j (m t) -> p m j t", t=PACK)
-            if e == LAST:
+            if ROUND1[e] == "S":
+                nc.scalar.copy(dst, src)
+            elif ROUND1[e] == "G":
+                nc.scalar.copy(dst[:, POOL_M:], src[:, POOL_M:])
+                nc.gpsimd.tensor_scalar(
+                    w1_bf[e][:].rearrange("p (t m j) -> p m t j", t=PACK, j=PACK)[:, :POOL_M],
+                    w1_raw[e][:].rearrange("p j (m t) -> p m t j", t=PACK)[:, :POOL_M],
+                    1.0,
+                    0.0,
+                    ALU.mult,
+                    ALU.add,
+                )
+            elif ROUND1[e] == "V":
+                nc.vector.tensor_copy(dst[:, :, :, 0:2], src[:, :, :, 0:2])
+                nc.vector.tensor_copy(dst[:, :, :, 2:4], src[:, :, :, 2:4])
+            else:
                 nc.vector.tensor_copy(dst[:, :, :, 0:2], src[:, :, :, 0:2])
                 nc.scalar.copy(dst[:, :, :, 2:4], src[:, :, :, 2:4])
-            elif scalar_rounds(e):
-                nc.scalar.copy(dst, src)
-            else:
-                nc.vector.tensor_copy(dst, src)
-
-        def quantised_with(e):
-            return e + 1 if e < LAST and not vector_rounds(e) and not scalar_rounds(e + 1) else e
 
         def quantise_w1(e):
-            if quantised_with(e) != e:
-                w1_q[e] = behind_rounding(e + 1, AT_CODES, [P, H], U32, "w1_q%d" % e)
+            if e in Q1_GATE:
+                w1_q[e] = behind_rounding(Q1_GATE[e], 6144, [P, H], U32, "w1_q%d" % e)
             else:
                 w1_q[e] = keep.tile([P, H], U32, name="w1_q%d" % e, align_bytes=64)
             w1_s[e] = keep.tile([P, H], U8, name="w1_s%d" % e, align_bytes=64)
-            width = H // 2 if e == LAST else H
+            width = H if ROUND1[e] in "SG" else H // 2
             for first in range(0, H, width):
                 cols = slice(first, first + width)
                 nc.vector.quantize_mx(
@@ -167,39 +185,42 @@ def tile_moe_ogt_gelu_silu_kernel(
                     in_=w1_bf[e][:, PACK * first : PACK * (first + width)],
                 )
 
-        def first_layer(e):
-            after = quantised_with(e) + 1
-            if after < E and scalar_rounds(after):
-                h_bf[e] = behind_rounding(after, AT_H_BF + e % 2 * 2 * PACK * C, [P, PACK * C], BF16, "h_bf%d" % e)
-            else:
-                h_bf[e] = keep.tile([P, PACK * C], BF16, name="h_bf%d" % e, align_bytes=64)
+        def first_product(e):
             a, first = divmod(e * C, PAIR)
             for u in range(C // P):
                 slots = slice(first + u * P, first + (u + 1) * P)
-                h_ps = bank([P, PACK, P], "h_ps", (2 * e + u) % 4)
+                h_ps[e, u] = bank([P, PACK, P], "h_ps", (2 * e + u) % 4)
                 for t in range(PACK):
                     cols = slice(t * P, (t + 1) * P)
                     nc.tensor.matmul_mx(
-                        out=h_ps[:, t, :],
+                        out=h_ps[e, u][:, t, :],
                         lhsT=w1_q[e][:, cols].bitcast(FP8X4),
                         lhsT_scale=w1_s[e][:, cols],
-                        rhs=xg_w[a][:, slots].bitcast(FP8X4),
+                        rhs=xg_w[e][:, u * P : (u + 1) * P].bitcast(FP8X4),
                         rhs_scale=xg_s[a][:, slots],
                         start=True,
                         stop=True,
                     )
+
+        def gelu(e):
+            if e in GELU_GATE:
+                h_bf[e] = behind_rounding(GELU_GATE[e], e % 2 * 2 * PACK * C, [P, PACK * C], BF16, "h_bf%d" % e)
+            else:
+                h_bf[e] = keep.tile([P, PACK * C], BF16, name="h_bf%d" % e, align_bytes=64)
+            for u in range(C // P):
                 nc.scalar.activation(
                     h_bf[e][:, u * PACK * P : (u + 1) * PACK * P].rearrange("p (n t) -> p n t", t=PACK),
-                    h_ps[:].rearrange("p t n -> p n t"),
+                    h_ps[e, u][:].rearrange("p t n -> p n t"),
                     ACT.Gelu_apprx_tanh,
                 )
 
         def quantise_h(e):
-            if h_waits_for(e) is not None:
-                h_q[e] = behind_rounding(h_waits_for(e), AT_H_Q + e % 2 * 4 * C, [P, C], U32, "h_q%d" % e)
+            if e in QH_GATE:
+                h_q[e] = behind_rounding(QH_GATE[e], AT_H_Q + e % 2 * 4 * C, [P, C], U32, "h_q%d" % e)
+            elif e in QH_TAG:
+                h_q[e] = keep.tile([P, C], U32, name="h_q%d" % e, tag="w2_bf%d" % QH_TAG[e], align_bytes=64)
             else:
-                tag = "w2_bf%d" % (e // 2) if e == LAST else "h_q%d" % e
-                h_q[e] = keep.tile([P, C], U32, name="h_q%d" % e, tag=tag, align_bytes=64)
+                h_q[e] = keep.tile([P, C], U32, name="h_q%d" % e, align_bytes=64)
             h_s[e] = keep.tile([P, C], U8, name="h_s%d" % e, align_bytes=64)
             width = P if e == LAST else C
             for first in range(0, C, width):
@@ -214,18 +235,26 @@ def tile_moe_ogt_gelu_silu_kernel(
             w2_bf[a] = keep.tile([P, 2 * PACK * N], BF16, name="w2_bf%d" % a, align_bytes=64)
             dst = w2_bf[a][:].rearrange("p (e c i j) -> p e c j i", e=2, i=PACK, j=PACK)
             src = w2_raw[a][:].rearrange("p e j (c i) -> p e c j i", i=PACK)
-            if a % 2 == 0:
+            if ROUND2[a] == "S":
                 nc.scalar.copy(dst, src)
             else:
-                nc.vector.tensor_copy(dst, src)
+                for b in range(2):
+                    nc.vector.tensor_copy(dst[:, b], src[:, b])
 
         def quantise_w2(a):
-            if a == 0:
-                w2_q[a] = behind_rounding(LAST, AT_CODES, [P, 2 * N], U32, "w2_q0")
+            if a in Q2_GATE:
+                w2_q[a] = behind_rounding(Q2_GATE[a], 7168, [P, 2 * N], U32, "w2_q%d" % a)
             else:
                 w2_q[a] = keep.tile([P, 2 * N], U32, name="w2_q%d" % a, align_bytes=64)
             w2_s[a] = keep.tile([P, 2 * N], U8, name="w2_s%d" % a, align_bytes=64)
-            nc.vector.quantize_mx(out=w2_q[a][:].bitcast(FP8X4), scales=w2_s[a][:], in_=w2_bf[a][:])
+            width = 2 * N if ROUND2[a] == "S" else N
+            for first in range(0, 2 * N, width):
+                cols = slice(first, first + width)
+                nc.vector.quantize_mx(
+                    out=w2_q[a][:, cols].bitcast(FP8X4),
+                    scales=w2_s[a][:, cols],
+                    in_=w2_bf[a][:, PACK * first : PACK * (first + width)],
+                )
 
         def second_product(y_ps, e, first, width):
             a, b = divmod(e, 2)
@@ -240,41 +269,52 @@ def tile_moe_ogt_gelu_silu_kernel(
             )
 
         def second_layer(a):
-            round_w2(a)
-            for e in (2 * a, 2 * a + 1):
-                if e not in h_q and e != LAST:
-                    quantise_h(e)
+            if a not in w2_bf:
+                round_w2(a)
             quantise_w2(a)
+            for e in range(E):
+                if e not in h_q and (QH_TAG.get(e) == a or e // 2 == a):
+                    quantise_h(e)
             if 2 * a + 1 < LAST:
                 y_ps = bank([P, PAIR], "y_ps", (4, 5, 0)[a])
                 for b in range(2):
                     second_product(y_ps[:, b * C : (b + 1) * C], 2 * a + b, 0, C)
-                nc.scalar.copy(y_sb[:, a * PAIR : (a + 1) * PAIR], y_ps[:])
+                if Y_ENG[a] == "S":
+                    nc.scalar.copy(y_sb[:, a * PAIR : (a + 1) * PAIR], y_ps[:])
+                else:
+                    nc.vector.tensor_copy(y_sb[:, a * PAIR : (a + 1) * PAIR], y_ps[:])
             else:
                 y_ps = bank([P, PAIR], "y_ps", 1)
                 second_product(y_ps[:, 0:C], LAST - 1, 0, C)
                 nc.vector.tensor_copy(y_sb[:, (LAST - 1) * C : LAST * C], y_ps[:, 0:C])
-                quantise_h(LAST)
                 for first, number in ((0, 4), (P, 2)):
                     y_ps = bank([P, PAIR], "y_ps", number)
                     cols = slice(C + first, C + first + P)
                     second_product(y_ps[:, cols], LAST, first, P)
                     nc.vector.tensor_copy(y_sb[:, LAST * C + first : LAST * C + first + P], y_ps[:, cols])
 
-        for a in range(2):
-            gather_tokens(a)
+        for a in range(E // 2):
+            gather_scales(a)
         for e in range(E):
             round_w1(e)
-            quantise_w1(e)
             for f in range(e):
-                if h_waits_for(f) == e:
+                if QH_TEXT.get(f) == e:
                     quantise_h(f)
-            if e < 2:
-                gather_tokens(e + 2)
-            first_layer(e)
-            if e == FIRST_W2_BEFORE - 1:
-                second_layer(0)
-        for a in range(1, E // 2):
+            quantise_w1(e)
+            if e == 0:
+                gather_words(0, 1)
+                gather_words(1, 1)
+            for first in (2, 4, 6):
+                if W_TEXT[first] == e:
+                    gather_words(first, 2)
+            for a in W2_TEXT:
+                if W2_TEXT[a] == e:
+                    round_w2(a)
+            first_product(e)
+            if e < LAST:
+                gelu(e)
+        gelu(LAST)
+        for a in range(E // 2):
             second_layer(a)
 
         gate_ps = bank([P, P], "gate_ps", 5)

@@ -24,31 +24,35 @@ PAIR = 2 * C
 LAST = E - 1
 BANK = 512
 
-ROUND1 = "SSSVSVVH"
-ROUND2 = "VVSV"
-POOL_M = 56
+GATHER_PHASE = 4
+POOLED = 2
 WORDS_AFTER = 2
-W2_BEFORE = {6: 0}
-GELU_GATE = {1: 2, 2: 4, 3: 4, 6: 7}
-QH_GATE = {2: 5, 3: 6, 4: 7, 5: 7}
-QH_TAG = {}
-QH_TEXT = {0: 3, 1: 3, 2: 5, 3: 6, 4: 7, 5: 7}
-W_GATE = {4: 1, 6: 1}
-Q1_GATE = {4: 5}
-Y_ENG = "SSSV"
-BF_CHAIN = ()
-Q2_GATE = {0: 7}
-W_BF = {}
-W_TEXT = {2: 0, 4: 1, 6: 1}
-W2_TEXT = {0: 5}
+FIRST_W2_BEFORE = 6
+SCALAR_W2 = 1
+H_LAG = 2
 TURNED = 512
 CHUNK = 256
 
 RAW = PACK * H * 4
-AT_WORDS = 0
+AT_H_BF = 0
+AT_WORDS = RAW // 2
 AT_H_Q = RAW // 2
+AT_CODES = 3 * RAW // 4
 AT_ROUNDED = E * RAW
-ROUNDED_STEP = 2560
+
+
+def scalar_alone(e):
+    return e < GATHER_PHASE and e != POOLED
+
+
+def halved(e):
+    return e >= GATHER_PHASE and e % 2 == 1
+
+
+def gelu_waits_for(e):
+    if 0 < e < GATHER_PHASE - 1:
+        return GATHER_PHASE - 1
+    return LAST if e == LAST - 1 else None
 
 
 def tile_moe_ogt_gelu_silu_kernel(
@@ -108,12 +112,11 @@ def tile_moe_ogt_gelu_silu_kernel(
         for e in range(E):
             if e == WORDS_AFTER:
                 nc.sync.dma_start(x_w[:], x_words[0].rearrange("p t d -> p (t d)").bitcast(I32))
-            if e in W2_BEFORE:
-                load_w2(W2_BEFORE[e])
+            if e == FIRST_W2_BEFORE:
+                load_w2(0)
             nc.sync.dma_start(w1_raw[e][:], w1[e].rearrange("(p j) c -> p j c", j=PACK))
-        for a in range(E // 2):
-            if a not in W2_BEFORE.values():
-                load_w2(a)
+        for a in range(1, E // 2):
+            load_w2(a)
         nc.sync.dma_start(wg_w[:].bitcast(I32), wg_words[0].bitcast(I32))
         for r in range(4):
             nc.sync.dma_start(wg_s[:].bitcast(I32)[r:P:32, :], wg_scales[0].bitcast(I32)[r:16:4, :])
@@ -123,60 +126,58 @@ def tile_moe_ogt_gelu_silu_kernel(
         for r in range(2):
             nc.sync.dma_start(gate_sb[r][:], gate[r][:, TURNED:])
 
-        w1_bf, w1_q, w1_s, xg_w, xg_s, h_bf, h_q, h_s, w2_bf, w2_q, w2_s, h_ps = ({} for i in range(12))
-
-        def behind_quantise(e, shape, dtype, name):
-            return reuse.tile(shape, dtype, name=name, align_bytes=64, offset=AT_ROUNDED + e * ROUNDED_STEP)
+        w1_bf, w1_q, w1_s, xg_w, xg_s, h_bf, h_q, h_s, w2_bf, w2_q, w2_s = ({} for i in range(11))
 
         def gather_scales(a):
             xg_s[a] = keep.tile([P, PAIR], U8, name="xg_s%d" % a, align_bytes=64)
             nc.vector.tensor_copy(xg_s[a][:], x_s[:].indirect(offs_sb[:, a * PAIR // 16 : (a + 1) * PAIR // 16]))
 
-        def gather_words(first, count):
-            if first in W_BF:
-                words = behind_quantise(W_BF[first], [P, count * C], U32, "xg_w%d" % first)
-            elif first in W_GATE:
-                words = behind_rounding(W_GATE[first], AT_WORDS + first // 2 % 2 * 8 * C, [P, count * C], U32, "xg_w%d" % first)
+        def gather_words(a):
+            if a < POOLED:
+                xg_w[a] = keep.tile([P, PAIR], U32, name="xg_w%d" % a, align_bytes=64)
             else:
-                words = keep.tile([P, count * C], U32, name="xg_w%d" % first, align_bytes=64)
-            entries = offs_sb[:, first * C // 16 : (first + count) * C // 16]
-            nc.vector.tensor_copy(words[:], x_w[:].bitcast(U32).indirect(entries))
-            for b in range(count):
-                xg_w[first + b] = words[:, b * C : (b + 1) * C]
+                xg_w[a] = behind_rounding(POOLED - 1, AT_WORDS + a % 2 * 4 * PAIR, [P, PAIR], U32, "xg_w%d" % a)
+            entries = offs_sb[:, a * PAIR // 16 : (a + 1) * PAIR // 16]
+            width = C if a == 0 else PAIR
+            for first in range(0, PAIR, width):
+                nc.vector.tensor_copy(
+                    xg_w[a][:, first : first + width],
+                    x_w[:].bitcast(U32).indirect(entries[:, first // 16 : (first + width) // 16]),
+                )
 
         def round_w1(e):
-            if e in BF_CHAIN:
-                w1_bf[e] = behind_quantise(e, [P, PACK * H], BF16, "w1_bf%d" % e)
+            if e in (POOLED - 1, POOLED):
+                w1_bf[e] = reuse.tile([P, PACK * H], BF16, name="w1_bf%d" % e, align_bytes=64, offset=AT_ROUNDED)
             else:
                 w1_bf[e] = keep.tile([P, PACK * H], BF16, name="w1_bf%d" % e, align_bytes=64)
             dst = w1_bf[e][:].rearrange("p (t m j) -> p m j t", t=PACK, j=PACK)
             src = w1_raw[e][:].rearrange("p j (m t) -> p m j t", t=PACK)
-            if ROUND1[e] == "S":
+            if scalar_alone(e):
                 nc.scalar.copy(dst, src)
-            elif ROUND1[e] == "G":
-                nc.scalar.copy(dst[:, POOL_M:], src[:, POOL_M:])
+            elif e == POOLED:
+                nc.scalar.copy(dst[:, P // 2 :], src[:, P // 2 :])
                 nc.gpsimd.tensor_scalar(
-                    w1_bf[e][:].rearrange("p (t m j) -> p m t j", t=PACK, j=PACK)[:, :POOL_M],
-                    w1_raw[e][:].rearrange("p j (m t) -> p m t j", t=PACK)[:, :POOL_M],
+                    w1_bf[e][:].rearrange("p (t m j) -> p m t j", t=PACK, j=PACK)[:, : P // 2],
+                    w1_raw[e][:].rearrange("p j (m t) -> p m t j", t=PACK)[:, : P // 2],
                     1.0,
                     0.0,
                     ALU.mult,
                     ALU.add,
                 )
-            elif ROUND1[e] == "V":
-                nc.vector.tensor_copy(dst[:, :, :, 0:2], src[:, :, :, 0:2])
-                nc.vector.tensor_copy(dst[:, :, :, 2:4], src[:, :, :, 2:4])
             else:
                 nc.vector.tensor_copy(dst[:, :, :, 0:2], src[:, :, :, 0:2])
-                nc.scalar.copy(dst[:, :, :, 2:4], src[:, :, :, 2:4])
+                if halved(e):
+                    nc.scalar.copy(dst[:, :, :, 2:4], src[:, :, :, 2:4])
+                else:
+                    nc.vector.tensor_copy(dst[:, :, :, 2:4], src[:, :, :, 2:4])
 
         def quantise_w1(e):
-            if e in Q1_GATE:
-                w1_q[e] = behind_rounding(Q1_GATE[e], 6144, [P, H], U32, "w1_q%d" % e)
+            if e == GATHER_PHASE - 1:
+                w1_q[e] = behind_rounding(e + 1, AT_CODES, [P, H], U32, "w1_q%d" % e)
             else:
                 w1_q[e] = keep.tile([P, H], U32, name="w1_q%d" % e, align_bytes=64)
             w1_s[e] = keep.tile([P, H], U8, name="w1_s%d" % e, align_bytes=64)
-            width = H if ROUND1[e] in "SG" else H // 2
+            width = H if e < GATHER_PHASE else H // 2
             for first in range(0, H, width):
                 cols = slice(first, first + width)
                 nc.vector.quantize_mx(
@@ -185,40 +186,36 @@ def tile_moe_ogt_gelu_silu_kernel(
                     in_=w1_bf[e][:, PACK * first : PACK * (first + width)],
                 )
 
-        def first_product(e):
+        def first_layer(e):
+            if gelu_waits_for(e) is not None:
+                at = AT_H_BF + e % 2 * 2 * PACK * C
+                h_bf[e] = behind_rounding(gelu_waits_for(e), at, [P, PACK * C], BF16, "h_bf%d" % e)
+            else:
+                h_bf[e] = keep.tile([P, PACK * C], BF16, name="h_bf%d" % e, align_bytes=64)
             a, first = divmod(e * C, PAIR)
             for u in range(C // P):
                 slots = slice(first + u * P, first + (u + 1) * P)
-                h_ps[e, u] = bank([P, PACK, P], "h_ps", (2 * e + u) % 4)
+                h_ps = bank([P, PACK, P], "h_ps", (2 * e + u) % 4)
                 for t in range(PACK):
                     cols = slice(t * P, (t + 1) * P)
                     nc.tensor.matmul_mx(
-                        out=h_ps[e, u][:, t, :],
+                        out=h_ps[:, t, :],
                         lhsT=w1_q[e][:, cols].bitcast(FP8X4),
                         lhsT_scale=w1_s[e][:, cols],
-                        rhs=xg_w[e][:, u * P : (u + 1) * P].bitcast(FP8X4),
+                        rhs=xg_w[a][:, slots].bitcast(FP8X4),
                         rhs_scale=xg_s[a][:, slots],
                         start=True,
                         stop=True,
                     )
-
-        def gelu(e):
-            if e in GELU_GATE:
-                h_bf[e] = behind_rounding(GELU_GATE[e], e % 2 * 2 * PACK * C, [P, PACK * C], BF16, "h_bf%d" % e)
-            else:
-                h_bf[e] = keep.tile([P, PACK * C], BF16, name="h_bf%d" % e, align_bytes=64)
-            for u in range(C // P):
                 nc.scalar.activation(
                     h_bf[e][:, u * PACK * P : (u + 1) * PACK * P].rearrange("p (n t) -> p n t", t=PACK),
-                    h_ps[e, u][:].rearrange("p t n -> p n t"),
+                    h_ps[:].rearrange("p t n -> p n t"),
                     ACT.Gelu_apprx_tanh,
                 )
 
         def quantise_h(e):
-            if e in QH_GATE:
-                h_q[e] = behind_rounding(QH_GATE[e], AT_H_Q + e % 2 * 4 * C, [P, C], U32, "h_q%d" % e)
-            elif e in QH_TAG:
-                h_q[e] = keep.tile([P, C], U32, name="h_q%d" % e, tag="w2_bf%d" % QH_TAG[e], align_bytes=64)
+            if e + H_LAG < E:
+                h_q[e] = behind_rounding(e + H_LAG, AT_H_Q, [P, C], U32, "h_q%d" % e)
             else:
                 h_q[e] = keep.tile([P, C], U32, name="h_q%d" % e, align_bytes=64)
             h_s[e] = keep.tile([P, C], U8, name="h_s%d" % e, align_bytes=64)
@@ -235,19 +232,19 @@ def tile_moe_ogt_gelu_silu_kernel(
             w2_bf[a] = keep.tile([P, 2 * PACK * N], BF16, name="w2_bf%d" % a, align_bytes=64)
             dst = w2_bf[a][:].rearrange("p (e c i j) -> p e c j i", e=2, i=PACK, j=PACK)
             src = w2_raw[a][:].rearrange("p e j (c i) -> p e c j i", i=PACK)
-            if ROUND2[a] == "S":
+            if a == SCALAR_W2:
                 nc.scalar.copy(dst, src)
             else:
                 for b in range(2):
                     nc.vector.tensor_copy(dst[:, b], src[:, b])
 
         def quantise_w2(a):
-            if a in Q2_GATE:
-                w2_q[a] = behind_rounding(Q2_GATE[a], 7168, [P, 2 * N], U32, "w2_q%d" % a)
+            if a == 0:
+                w2_q[a] = behind_rounding(LAST, AT_CODES, [P, 2 * N], U32, "w2_q0")
             else:
                 w2_q[a] = keep.tile([P, 2 * N], U32, name="w2_q%d" % a, align_bytes=64)
             w2_s[a] = keep.tile([P, 2 * N], U8, name="w2_s%d" % a, align_bytes=64)
-            width = 2 * N if ROUND2[a] == "S" else N
+            width = 2 * N if a == SCALAR_W2 else N
             for first in range(0, 2 * N, width):
                 cols = slice(first, first + width)
                 nc.vector.quantize_mx(
@@ -269,51 +266,36 @@ def tile_moe_ogt_gelu_silu_kernel(
             )
 
         def second_layer(a):
-            if a not in w2_bf:
+            if a > 0:
                 round_w2(a)
             quantise_w2(a)
-            for e in range(E):
-                if e not in h_q and (QH_TAG.get(e) == a or e // 2 == a):
-                    quantise_h(e)
             if 2 * a + 1 < LAST:
                 y_ps = bank([P, PAIR], "y_ps", (4, 5, 0)[a])
                 for b in range(2):
                     second_product(y_ps[:, b * C : (b + 1) * C], 2 * a + b, 0, C)
-                if Y_ENG[a] == "S":
-                    nc.scalar.copy(y_sb[:, a * PAIR : (a + 1) * PAIR], y_ps[:])
-                else:
-                    nc.vector.tensor_copy(y_sb[:, a * PAIR : (a + 1) * PAIR], y_ps[:])
+                nc.scalar.copy(y_sb[:, a * PAIR : (a + 1) * PAIR], y_ps[:])
             else:
-                y_ps = bank([P, PAIR], "y_ps", 1)
-                second_product(y_ps[:, 0:C], LAST - 1, 0, C)
-                nc.vector.tensor_copy(y_sb[:, (LAST - 1) * C : LAST * C], y_ps[:, 0:C])
-                for first, number in ((0, 4), (P, 2)):
-                    y_ps = bank([P, PAIR], "y_ps", number)
-                    cols = slice(C + first, C + first + P)
-                    second_product(y_ps[:, cols], LAST, first, P)
-                    nc.vector.tensor_copy(y_sb[:, LAST * C + first : LAST * C + first + P], y_ps[:, cols])
+                quantise_h(LAST - 1)
+                quantise_h(LAST)
+                for e, first, width, number in ((LAST - 1, 0, C, 1), (LAST, 0, P, 4), (LAST, P, P, 2)):
+                    y_ps = bank([P, width], "y_ps", number)
+                    second_product(y_ps[:], e, first, width)
+                    nc.vector.tensor_copy(y_sb[:, e * C + first : e * C + first + width], y_ps[:])
 
         for a in range(E // 2):
             gather_scales(a)
         for e in range(E):
             round_w1(e)
-            for f in range(e):
-                if QH_TEXT.get(f) == e:
+            for f in range(E - H_LAG):
+                if min(f + H_LAG + 1, LAST) == e:
                     quantise_h(f)
             quantise_w1(e)
-            if e == 0:
-                gather_words(0, 1)
-                gather_words(1, 1)
-            for first in (2, 4, 6):
-                if W_TEXT[first] == e:
-                    gather_words(first, 2)
-            for a in W2_TEXT:
-                if W2_TEXT[a] == e:
-                    round_w2(a)
-            first_product(e)
-            if e < LAST:
-                gelu(e)
-        gelu(LAST)
+            if e < 2:
+                gather_words(2 * e)
+                gather_words(2 * e + 1)
+            if e == FIRST_W2_BEFORE - 1:
+                round_w2(0)
+            first_layer(e)
         for a in range(E // 2):
             second_layer(a)
 

@@ -30,7 +30,7 @@ WORDS_AFTER = 2
 FIRST_W2_BEFORE = 6
 SCALAR_W2 = 1
 H_LAG = 2
-TURNED = 512
+TURNED = 768
 CHUNK = 256
 
 RAW = PACK * H * 4
@@ -62,7 +62,6 @@ def tile_moe_ogt_gelu_silu_kernel(
     with ExitStack() as ctx:
         keep = ctx.enter_context(tc.tile_pool(name="keep", bufs=1))
         reuse = ctx.enter_context(tc.tile_pool(name="reuse", bufs=1))
-        ring = ctx.enter_context(tc.tile_pool(name="ring", bufs=2))
         psum = ctx.enter_context(tc.psum_pool(name="psum", bufs=1))
 
         offs_sb = keep.tile([P, SLOTS // 16], U16, name="offs_sb")
@@ -75,9 +74,7 @@ def tile_moe_ogt_gelu_silu_kernel(
             reuse.tile([P, PACK, H], F32, name="w1_raw%d" % e, align_bytes=64, offset=e * RAW) for e in range(E)
         ]
         w2_raw = [keep.tile([P, 2, PACK, N], F32, name="w2_raw%d" % a, align_bytes=64) for a in range(E // 2)]
-        gate_rows = keep.tile([P, P], F32, name="gate_rows")
-        gate_cols = keep.tile([P, 2 * T // P], F32, name="gate_cols")
-        gate_sb = [keep.tile([P, T - TURNED], F32, name="gate%d_sb" % r) for r in range(2)]
+        gate_sb = [keep.tile([P, 2, CHUNK], F32, name="gate%d" % c) for c in range(T // CHUNK)]
         ident = keep.tile([P, P], F32, name="ident")
         make_identity(nc, ident[:])
         y_sb = keep.tile([P, SLOTS], F32, name="y_sb")
@@ -86,7 +83,6 @@ def tile_moe_ogt_gelu_silu_kernel(
 
         nc.vector.memset(wg_s[:].bitcast(I32), 0)
         nc.vector.memset(warm[:], 0.0)
-        nc.vector.memset(gate_rows[:], 0.0)
 
         def bank(shape, name, number):
             return psum.tile(shape, F32, name=name, tag="bank%d" % number)
@@ -120,11 +116,10 @@ def tile_moe_ogt_gelu_silu_kernel(
         nc.sync.dma_start(wg_w[:].bitcast(I32), wg_words[0].bitcast(I32))
         for r in range(4):
             nc.sync.dma_start(wg_s[:].bitcast(I32)[r:P:32, :], wg_scales[0].bitcast(I32)[r:16:4, :])
-        nc.sync.dma_start(gate_rows[0:16, :], gate[:, 0, :].rearrange("r (c q) -> r c q", q=P))
         nc.sync.dma_start(pos_sb[0][:], pos1)
         nc.sync.dma_start(pos_sb[1][:], pos2)
-        for r in range(2):
-            nc.sync.dma_start(gate_sb[r][:], gate[r][:, TURNED:])
+        for c in range(T // CHUNK):
+            nc.sync.dma_start(gate_sb[c][:], gate[:, :, c * CHUNK : (c + 1) * CHUNK].rearrange("r p t -> p r t"))
 
         w1_bf, w1_q, w1_s, xg_w, xg_s, h_bf, h_q, h_s, w2_bf, w2_q, w2_s = ({} for i in range(11))
 
@@ -299,10 +294,6 @@ def tile_moe_ogt_gelu_silu_kernel(
         for a in range(E // 2):
             second_layer(a)
 
-        gate_ps = bank([P, P], "gate_ps", 5)
-        nc.tensor.transpose(gate_ps[:], gate_rows[:], ident[:])
-        nc.scalar.copy(gate_cols[:], gate_ps[:, : 2 * T // P])
-
         o_sb = keep.tile([P, T], F32, name="o_sb", tag="h_bf%d" % LAST, align_bytes=64)
         for u in range(T // BANK):
             tokens = slice(u * BANK, (u + 1) * BANK)
@@ -318,50 +309,46 @@ def tile_moe_ogt_gelu_silu_kernel(
             )
             nc.scalar.activation(o_sb[:, tokens], o_ps[:], ACT.Silu)
 
-        totals = []
-        for c in range(TURNED // CHUNK):
-            scaled = ring.tile([P, 2, CHUNK], F32, name="scaled")
-            for r in range(2):
-                picked = ring.tile([P, CHUNK], F32, name="picked", bufs=2 * TURNED // CHUNK)
-                entries = pos_sb[r][:, c * CHUNK // 16 : (c + 1) * CHUNK // 16]
-                nc.vector.tensor_copy(picked[:], y_sb[:].indirect(entries))
-                turned = bank([P, CHUNK], "turned", 2 * c + r)
-                for b in range(CHUNK // P):
-                    cols = slice(b * P, (b + 1) * P)
-                    nc.tensor.transpose(turned[:, cols], picked[:, cols], ident[:])
-                for b in range(CHUNK // P):
-                    cols = slice(b * P, (b + 1) * P)
-                    g = r * (T // P) + c * (CHUNK // P) + b
-                    nc.scalar.activation(scaled[:, r, cols], turned[:, cols], ACT.Copy, scale=gate_cols[:, g : g + 1])
-            total = bank([P, CHUNK], "total", 4 + c)
-            for b in range(CHUNK // P):
-                cols = slice(b * P, (b + 1) * P)
-                for r in range(2):
-                    nc.tensor.matmul(
-                        total[:, cols], scaled[:, r, cols], ident[:], is_transpose=True, start=(r == 0), stop=(r == 1)
-                    )
-            totals.append(total)
-
-        for t0 in range(TURNED, T, CHUNK):
-            t1 = t0 + CHUNK
+        def weighted(t0):
             parts = []
             for r in range(2):
                 part = keep.tile([P, CHUNK], F32, name="part%d_%d" % (t0, r))
                 nc.vector.tensor_tensor(
                     part[:],
-                    y_sb[:].indirect(pos_sb[r][:, t0 // 16 : t1 // 16]),
-                    gate_sb[r][:, t0 - TURNED : t1 - TURNED],
+                    y_sb[:].indirect(pos_sb[r][:, t0 // 16 : (t0 + CHUNK) // 16]),
+                    gate_sb[t0 // CHUNK][:, r, :],
                     ALU.mult,
                 )
                 parts.append(part)
-            both = keep.tile([P, CHUNK], F32, name="both%d" % t0)
-            nc.vector.tensor_tensor(both[:], parts[0][:], parts[1][:], ALU.add)
-            gated = keep.tile([P, CHUNK], F32, name="gated%d" % t0)
-            nc.vector.tensor_tensor(gated[:], both[:], o_sb[:, t0:t1], ALU.mult)
-            nc.sync.dma_start(out[:, t0:t1], gated[:])
+            return parts
 
+        def finish(t0, total):
+            result = keep.tile([P, CHUNK], F32, name="result%d" % t0)
+            nc.vector.tensor_tensor(result[:], total, o_sb[:, t0 : t0 + CHUNK], ALU.mult)
+            nc.sync.dma_start(out[:, t0 : t0 + CHUNK], result[:])
+
+        totals = []
         for c in range(TURNED // CHUNK):
-            tokens = slice(c * CHUNK, (c + 1) * CHUNK)
-            result = keep.tile([P, CHUNK], F32, name="result%d" % c)
-            nc.vector.tensor_tensor(result[:], totals[c][:], o_sb[:, tokens], ALU.mult)
-            nc.sync.dma_start(out[:, tokens], result[:])
+            parts = weighted(c * CHUNK)
+            turned = bank([P, CHUNK], "turned", c)
+            for b in range(CHUNK // P):
+                cols = slice(b * P, (b + 1) * P)
+                for r in range(2):
+                    nc.tensor.matmul(
+                        turned[:, cols], parts[r][:, cols], ident[:], is_transpose=True, start=(r == 0), stop=(r == 1)
+                    )
+            summed = keep.tile([P, CHUNK], F32, name="summed%d" % c)
+            nc.scalar.copy(summed[:], turned[:])
+            total = bank([P, CHUNK], "total", 3 + c)
+            for b in range(CHUNK // P):
+                cols = slice(b * P, (b + 1) * P)
+                nc.tensor.transpose(total[:, cols], summed[:, cols], ident[:])
+            totals.append(total)
+
+        parts = weighted(TURNED)
+        finish(0, totals[0][:])
+        both = keep.tile([P, CHUNK], F32, name="both")
+        nc.vector.tensor_tensor(both[:], parts[0][:], parts[1][:], ALU.add)
+        finish(CHUNK, totals[1][:])
+        finish(TURNED, both[:])
+        finish(2 * CHUNK, totals[2][:])

@@ -28,7 +28,6 @@ GATHER_PHASE = 4
 POOLED = 2
 WORDS_AFTER = 2
 FIRST_W2_BEFORE = 6
-SCALAR_W2 = 1
 H_LAG = 2
 TURNED = 768
 CHUNK = 256
@@ -172,7 +171,7 @@ def tile_moe_ogt_gelu_silu_kernel(
             else:
                 w1_q[e] = keep.tile([P, H], U32, name="w1_q%d" % e, align_bytes=64)
             w1_s[e] = keep.tile([P, H], U8, name="w1_s%d" % e, align_bytes=64)
-            width = H if e < GATHER_PHASE else H // 2
+            width = H if e < GATHER_PHASE or halved(e) else H // 2
             for first in range(0, H, width):
                 cols = slice(first, first + width)
                 nc.vector.quantize_mx(
@@ -227,25 +226,21 @@ def tile_moe_ogt_gelu_silu_kernel(
             w2_bf[a] = keep.tile([P, 2 * PACK * N], BF16, name="w2_bf%d" % a, align_bytes=64)
             dst = w2_bf[a][:].rearrange("p (e c i j) -> p e c j i", e=2, i=PACK, j=PACK)
             src = w2_raw[a][:].rearrange("p e j (c i) -> p e c j i", i=PACK)
-            if a == SCALAR_W2:
-                nc.scalar.copy(dst, src)
-            else:
-                for b in range(2):
+            for b in range(2):
+                if b == 1 and 0 < a < E // 2 - 1:
+                    nc.scalar.copy(dst[:, b], src[:, b])
+                else:
                     nc.vector.tensor_copy(dst[:, b], src[:, b])
 
         def quantise_w2(a):
-            if a == 0:
-                w2_q[a] = behind_rounding(LAST, AT_CODES, [P, 2 * N], U32, "w2_q0")
-            else:
-                w2_q[a] = keep.tile([P, 2 * N], U32, name="w2_q%d" % a, align_bytes=64)
+            w2_q[a] = keep.tile([P, 2 * N], U32, name="w2_q%d" % a, align_bytes=64)
             w2_s[a] = keep.tile([P, 2 * N], U8, name="w2_s%d" % a, align_bytes=64)
-            width = 2 * N if a == SCALAR_W2 else N
-            for first in range(0, 2 * N, width):
-                cols = slice(first, first + width)
+            for first in range(0, 2 * N, N):
+                cols = slice(first, first + N)
                 nc.vector.quantize_mx(
                     out=w2_q[a][:, cols].bitcast(FP8X4),
                     scales=w2_s[a][:, cols],
-                    in_=w2_bf[a][:, PACK * first : PACK * (first + width)],
+                    in_=w2_bf[a][:, PACK * first : PACK * (first + N)],
                 )
 
         def second_product(y_ps, e, first, width):
@@ -275,7 +270,11 @@ def tile_moe_ogt_gelu_silu_kernel(
                 for e, first, width, number in ((LAST - 1, 0, C, 1), (LAST, 0, P, 4), (LAST, P, P, 2)):
                     y_ps = bank([P, width], "y_ps", number)
                     second_product(y_ps[:], e, first, width)
-                    nc.vector.tensor_copy(y_sb[:, e * C + first : e * C + first + width], y_ps[:])
+                    slots = slice(e * C + first, e * C + first + width)
+                    if first == 0:
+                        nc.vector.tensor_copy(y_sb[:, slots], y_ps[:])
+                    else:
+                        nc.scalar.copy(y_sb[:, slots], y_ps[:])
 
         for a in range(E // 2):
             gather_scales(a)
@@ -291,7 +290,9 @@ def tile_moe_ogt_gelu_silu_kernel(
             if e == FIRST_W2_BEFORE - 1:
                 round_w2(0)
             first_layer(e)
-        for a in range(E // 2):
+            if e == FIRST_W2_BEFORE - 1:
+                second_layer(0)
+        for a in range(1, E // 2):
             second_layer(a)
 
         o_sb = keep.tile([P, T], F32, name="o_sb", tag="h_bf%d" % LAST, align_bytes=64)

@@ -158,12 +158,12 @@ def tile_moe_ogt_gelu_silu_kernel(
                     ALU.mult,
                     ALU.add,
                 )
+            elif halved(e):
+                nc.vector.tensor_copy(dst[:, : P // 2], src[:, : P // 2])
+                nc.scalar.copy(dst[:, P // 2 :], src[:, P // 2 :])
             else:
                 nc.vector.tensor_copy(dst[:, :, :, 0:2], src[:, :, :, 0:2])
-                if halved(e):
-                    nc.scalar.copy(dst[:, :, :, 2:4], src[:, :, :, 2:4])
-                else:
-                    nc.vector.tensor_copy(dst[:, :, :, 2:4], src[:, :, :, 2:4])
+                nc.vector.tensor_copy(dst[:, :, :, 2:4], src[:, :, :, 2:4])
 
         def quantise_w1(e):
             if e == GATHER_PHASE - 1:

@@ -1,7 +1,6 @@
 from contextlib import ExitStack
 
 import concourse.mybir as mybir
-from concourse.masks import make_identity
 
 K, T, E, C, H, N = 512, 1024, 8, 256, 512, 128
 SLOTS = E * C
@@ -29,7 +28,6 @@ POOLED = 2
 WORDS_AFTER = 2
 FIRST_W2_BEFORE = 6
 H_LAG = 2
-TURNED = 768
 CHUNK = 256
 
 RAW = PACK * H * 4
@@ -74,8 +72,6 @@ def tile_moe_ogt_gelu_silu_kernel(
         ]
         w2_raw = [keep.tile([P, 2, PACK, N], F32, name="w2_raw%d" % a, align_bytes=64) for a in range(E // 2)]
         gate_sb = [keep.tile([P, 2, CHUNK], F32, name="gate%d" % c) for c in range(T // CHUNK)]
-        ident = keep.tile([P, P], F32, name="ident")
-        make_identity(nc, ident[:])
         y_sb = keep.tile([P, SLOTS], F32, name="y_sb")
         warm = keep.tile([P, 8], F32, name="warm")
         warm_out = keep.tile([P, 8], F32, name="warm_out")
@@ -271,10 +267,7 @@ def tile_moe_ogt_gelu_silu_kernel(
                     y_ps = bank([P, width], "y_ps", number)
                     second_product(y_ps[:], e, first, width)
                     slots = slice(e * C + first, e * C + first + width)
-                    if first == 0:
-                        nc.vector.tensor_copy(y_sb[:, slots], y_ps[:])
-                    else:
-                        nc.scalar.copy(y_sb[:, slots], y_ps[:])
+                    nc.vector.tensor_copy(y_sb[:, slots], y_ps[:])
 
         for a in range(E // 2):
             gather_scales(a)
@@ -310,46 +303,49 @@ def tile_moe_ogt_gelu_silu_kernel(
             )
             nc.scalar.activation(o_sb[:, tokens], o_ps[:], ACT.Silu)
 
-        def weighted(t0):
-            parts = []
-            for r in range(2):
-                part = keep.tile([P, CHUNK], F32, name="part%d_%d" % (t0, r))
-                nc.vector.tensor_tensor(
-                    part[:],
-                    y_sb[:].indirect(pos_sb[r][:, t0 // 16 : (t0 + CHUNK) // 16]),
-                    gate_sb[t0 // CHUNK][:, r, :],
-                    ALU.mult,
-                )
-                parts.append(part)
-            return parts
+        parts, plain, total = ({} for i in range(3))
 
-        def finish(t0, total):
-            result = keep.tile([P, CHUNK], F32, name="result%d" % t0)
-            nc.vector.tensor_tensor(result[:], total, o_sb[:, t0 : t0 + CHUNK], ALU.mult)
-            nc.sync.dma_start(out[:, t0 : t0 + CHUNK], result[:])
+        def entries(r, c):
+            return pos_sb[r][:, c * CHUNK // 16 : (c + 1) * CHUNK // 16]
 
-        totals = []
-        for c in range(TURNED // CHUNK):
-            parts = weighted(c * CHUNK)
-            turned = bank([P, CHUNK], "turned", c)
-            for b in range(CHUNK // P):
-                cols = slice(b * P, (b + 1) * P)
-                for r in range(2):
-                    nc.tensor.matmul(
-                        turned[:, cols], parts[r][:, cols], ident[:], is_transpose=True, start=(r == 0), stop=(r == 1)
-                    )
-            summed = keep.tile([P, CHUNK], F32, name="summed%d" % c)
-            nc.scalar.copy(summed[:], turned[:])
-            total = bank([P, CHUNK], "total", 3 + c)
-            for b in range(CHUNK // P):
-                cols = slice(b * P, (b + 1) * P)
-                nc.tensor.transpose(total[:, cols], summed[:, cols], ident[:])
-            totals.append(total)
+        def fetch(r, c):
+            plain[r, c] = keep.tile([P, CHUNK], F32, name="plain%d_%d" % (r, c))
+            nc.scalar.activation(plain[r, c][:], y_sb[:].indirect(entries(r, c)), ACT.Copy)
 
-        parts = weighted(TURNED)
-        finish(0, totals[0][:])
-        both = keep.tile([P, CHUNK], F32, name="both")
-        nc.vector.tensor_tensor(both[:], parts[0][:], parts[1][:], ALU.add)
-        finish(CHUNK, totals[1][:])
-        finish(TURNED, both[:])
-        finish(2 * CHUNK, totals[2][:])
+        def fetch_weighted(r, c):
+            parts[r, c] = keep.tile([P, CHUNK], F32, name="part%d_%d" % (r, c))
+            nc.vector.tensor_tensor(parts[r, c][:], y_sb[:].indirect(entries(r, c)), gate_sb[c][:, r, :], ALU.mult)
+
+        def weigh(r, c):
+            parts[r, c] = keep.tile([P, CHUNK], F32, name="part%d_%d" % (r, c))
+            nc.vector.tensor_tensor(parts[r, c][:], plain[r, c][:], gate_sb[c][:, r, :], ALU.mult)
+
+        def add(c, cols):
+            if cols.start == 0:
+                total[c] = keep.tile([P, CHUNK], F32, name="both%d" % c)
+            nc.vector.tensor_tensor(total[c][:, cols], parts[0, c][:, cols], parts[1, c][:, cols], ALU.add)
+
+        def finish(c, pieces):
+            result = keep.tile([P, CHUNK], F32, name="result%d" % c)
+            for cols in pieces:
+                nc.vector.tensor_tensor(result[:, cols], total[c][:, cols], o_sb[:, c * CHUNK :][:, cols], ALU.mult)
+            nc.sync.dma_start(out[:, c * CHUNK : (c + 1) * CHUNK], result[:])
+
+        whole, halves = slice(0, CHUNK), (slice(0, P), slice(P, CHUNK))
+        for c in range(4):
+            fetch(1, c)
+        fetch(0, 3)
+        for c in range(3):
+            fetch_weighted(0, c)
+        weigh(1, 0)
+        add(0, whole)
+        for c in range(1, 3):
+            weigh(1, c)
+            finish(c - 1, [whole])
+            add(c, whole)
+        weigh(1, 3)
+        weigh(0, 3)
+        finish(2, [whole])
+        for cols in halves:
+            add(3, cols)
+        finish(3, halves)

@@ -1,6 +1,7 @@
 from contextlib import ExitStack
 
 import concourse.mybir as mybir
+from concourse.masks import make_identity
 
 K, T, E, C, H, N = 512, 1024, 8, 256, 512, 128
 SLOTS = E * C
@@ -28,6 +29,7 @@ POOLED = 2
 WORDS_AFTER = 2
 FIRST_W2_BEFORE = 6
 H_LAG = 2
+TURNED = 2
 CHUNK = 256
 
 RAW = PACK * H * 4
@@ -72,6 +74,8 @@ def tile_moe_ogt_gelu_silu_kernel(
         ]
         w2_raw = [keep.tile([P, 2, PACK, N], F32, name="w2_raw%d" % a, align_bytes=64) for a in range(E // 2)]
         gate_sb = [keep.tile([P, 2, CHUNK], F32, name="gate%d" % c) for c in range(T // CHUNK)]
+        ident = keep.tile([P, P], F32, name="ident")
+        make_identity(nc, ident[:])
         y_sb = keep.tile([P, SLOTS], F32, name="y_sb")
         warm = keep.tile([P, 8], F32, name="warm")
         warm_out = keep.tile([P, 8], F32, name="warm_out")
@@ -288,20 +292,39 @@ def tile_moe_ogt_gelu_silu_kernel(
         for a in range(1, E // 2):
             second_layer(a)
 
-        o_sb = keep.tile([P, T], F32, name="o_sb", tag="h_bf%d" % LAST, align_bytes=64)
-        for u in range(T // BANK):
-            tokens = slice(u * BANK, (u + 1) * BANK)
-            o_ps = bank([P, BANK], "o_ps", 6 + u)
+        half = TURNED * CHUNK
+
+        def output_gate_turned():
+            o_tile = keep.tile([P, half], F32, name="o_turned", tag="h_bf%d" % LAST, align_bytes=64)
+            o_ps = bank([P, half], "o_ps", 6)
+            for b in range(half // P):
+                block = slice(b * P, (b + 1) * P)
+                nc.tensor.matmul_mx(
+                    out=o_ps[:, block],
+                    lhsT=x_w[:, block].bitcast(FP8X4),
+                    lhsT_scale=x_s[:, block],
+                    rhs=wg_w[:].bitcast(FP4X4),
+                    rhs_scale=wg_s[:],
+                    start=True,
+                    stop=True,
+                )
+            nc.scalar.activation(o_tile[:], o_ps[:], ACT.Silu)
+            return o_tile
+
+        def output_gate_plain():
+            o_tile = keep.tile([P, T - half], F32, name="o_plain")
+            o_ps = bank([P, T - half], "o_ps", 2)
             nc.tensor.matmul_mx(
                 out=o_ps[:],
                 lhsT=wg_w[:].bitcast(FP4X4),
                 lhsT_scale=wg_s[:],
-                rhs=x_w[:, tokens].bitcast(FP8X4),
-                rhs_scale=x_s[:, tokens],
+                rhs=x_w[:, half:].bitcast(FP8X4),
+                rhs_scale=x_s[:, half:],
                 start=True,
                 stop=True,
             )
-            nc.scalar.activation(o_sb[:, tokens], o_ps[:], ACT.Silu)
+            nc.scalar.activation(o_tile[:], o_ps[:], ACT.Silu)
+            return o_tile
 
         parts, plain, total = ({} for i in range(3))
 
@@ -320,32 +343,62 @@ def tile_moe_ogt_gelu_silu_kernel(
             parts[r, c] = keep.tile([P, CHUNK], F32, name="part%d_%d" % (r, c))
             nc.vector.tensor_tensor(parts[r, c][:], plain[r, c][:], gate_sb[c][:, r, :], ALU.mult)
 
-        def add(c, cols):
-            if cols.start == 0:
-                total[c] = keep.tile([P, CHUNK], F32, name="both%d" % c)
-            nc.vector.tensor_tensor(total[c][:, cols], parts[0, c][:, cols], parts[1, c][:, cols], ALU.add)
+        def add_turned(c):
+            total[c] = bank([P, CHUNK], "turned", c)
+            for b in range(CHUNK // P):
+                cols = slice(b * P, (b + 1) * P)
+                for r in range(2):
+                    nc.tensor.matmul(
+                        total[c][:, cols], parts[r, c][:, cols], ident[:], is_transpose=True, start=(r == 0), stop=(r == 1)
+                    )
 
-        def finish(c, pieces):
+        def finish_turned(c, o_tile):
+            scaled = keep.tile([P, CHUNK], F32, name="scaled%d" % c)
+            nc.vector.tensor_tensor(scaled[:], total[c][:], o_tile[:, c * CHUNK : (c + 1) * CHUNK], ALU.mult)
+            back = bank([P, CHUNK], "back", 3 + 2 * c)
+            for b in range(CHUNK // P):
+                cols = slice(b * P, (b + 1) * P)
+                nc.tensor.transpose(back[:, cols], scaled[:, cols], ident[:])
+            return back
+
+        def store_turned(c, back):
             result = keep.tile([P, CHUNK], F32, name="result%d" % c)
-            for cols in pieces:
-                nc.vector.tensor_tensor(result[:, cols], total[c][:, cols], o_sb[:, c * CHUNK :][:, cols], ALU.mult)
+            nc.scalar.copy(result[:], back[:])
+            nc.scalar.dma_start(out[:, c * CHUNK : (c + 1) * CHUNK], result[:])
+
+        def pieces(c):
+            width = CHUNK if (c + 1) * CHUNK < T else P
+            return [slice(first, first + width) for first in range(0, CHUNK, width)]
+
+        def add(c):
+            total[c] = keep.tile([P, CHUNK], F32, name="both%d" % c)
+            for cols in pieces(c):
+                nc.vector.tensor_tensor(total[c][:, cols], parts[0, c][:, cols], parts[1, c][:, cols], ALU.add)
+
+        def finish(c, o_tile):
+            result = keep.tile([P, CHUNK], F32, name="result%d" % c)
+            o_chunk = o_tile[:, (c - TURNED) * CHUNK : (c - TURNED + 1) * CHUNK]
+            for cols in pieces(c):
+                nc.vector.tensor_tensor(result[:, cols], total[c][:, cols], o_chunk[:, cols], ALU.mult)
             nc.sync.dma_start(out[:, c * CHUNK : (c + 1) * CHUNK], result[:])
 
-        whole, halves = slice(0, CHUNK), (slice(0, P), slice(P, CHUNK))
-        for c in range(4):
-            fetch(1, c)
-        fetch(0, 3)
-        for c in range(3):
+        o_turned = output_gate_turned()
+        for c in range(TURNED):
             fetch_weighted(0, c)
-        weigh(1, 0)
-        add(0, whole)
-        for c in range(1, 3):
-            weigh(1, c)
-            finish(c - 1, [whole])
-            add(c, whole)
-        weigh(1, 3)
+            fetch_weighted(1, c)
+            add_turned(c)
+        for c in range(TURNED, T // CHUNK):
+            fetch(0, c)
+            fetch(1, c)
+        o_plain = output_gate_plain()
+        backs = [finish_turned(c, o_turned) for c in range(TURNED)]
+        weigh(0, 2)
+        weigh(1, 2)
         weigh(0, 3)
-        finish(2, [whole])
-        for cols in halves:
-            add(3, cols)
-        finish(3, halves)
+        add(2)
+        weigh(1, 3)
+        finish(2, o_plain)
+        add(3)
+        for c in range(TURNED):
+            store_turned(c, backs[c])
+        finish(3, o_plain)

@@ -227,7 +227,7 @@ def tile_moe_ogt_gelu_silu_kernel(
             dst = w2_bf[a][:].rearrange("p (e c i j) -> p e c j i", e=2, i=PACK, j=PACK)
             src = w2_raw[a][:].rearrange("p e j (c i) -> p e c j i", i=PACK)
             for b in range(2):
-                if b == 1 and 0 < a < E // 2 - 1:
+                if b == 1 and a == 1:
                     nc.scalar.copy(dst[:, b], src[:, b])
                 else:
                     nc.vector.tensor_copy(dst[:, b], src[:, b])
@@ -295,8 +295,8 @@ def tile_moe_ogt_gelu_silu_kernel(
         half = TURNED * CHUNK
 
         def output_gate_turned():
-            o_tile = keep.tile([P, half], F32, name="o_turned", tag="h_bf%d" % LAST, align_bytes=64)
-            o_ps = bank([P, half], "o_ps", 6)
+            o_tile = keep.tile([P, half], F32, name="o_turned")
+            o_ps = bank([P, half], "o_ps", 0)
             for b in range(half // P):
                 block = slice(b * P, (b + 1) * P)
                 nc.tensor.matmul_mx(
@@ -344,7 +344,7 @@ def tile_moe_ogt_gelu_silu_kernel(
             nc.vector.tensor_tensor(parts[r, c][:], plain[r, c][:], gate_sb[c][:, r, :], ALU.mult)
 
         def add_turned(c):
-            total[c] = bank([P, CHUNK], "turned", c)
+            total[c] = bank([P, CHUNK], "turned", 6 + c)
             for b in range(CHUNK // P):
                 cols = slice(b * P, (b + 1) * P)
                 for r in range(2):

@@ -89,13 +89,13 @@ def tile_moe_ogt_gelu_silu_kernel(
         def behind_rounding(e, at, shape, dtype, name):
             return reuse.tile(shape, dtype, name=name, align_bytes=64, offset=e * RAW + at)
 
-        nc.sync.dma_start(offs_sb[:], offs)
         for q in range(4):
             queue = nc.sync if q < 2 else nc.scalar
             queue.dma_start(
                 x_s[:].bitcast(I32)[32 * q : 32 * q + 32, :],
                 x_scales[0].bitcast(I32)[4 * q : 4 * q + 4, :].partition_broadcast(8),
             )
+        nc.sync.dma_start(offs_sb[:], offs)
         nc.scalar.activation(warm_out[:], warm[:], ACT.Gelu_apprx_tanh)
 
         def load_w2(a):
@@ -171,7 +171,7 @@ def tile_moe_ogt_gelu_silu_kernel(
             else:
                 w1_q[e] = keep.tile([P, H], U32, name="w1_q%d" % e, align_bytes=64)
             w1_s[e] = keep.tile([P, H], U8, name="w1_s%d" % e, align_bytes=64)
-            width = H if e < GATHER_PHASE or halved(e) else H // 2
+            width = H if e < GATHER_PHASE or (halved(e) and e < LAST) else H // 2
             for first in range(0, H, width):
                 cols = slice(first, first + width)
                 nc.vector.quantize_mx(
@@ -277,10 +277,11 @@ def tile_moe_ogt_gelu_silu_kernel(
             gather_scales(a)
         for e in range(E):
             round_w1(e)
-            for f in range(E - H_LAG):
-                if min(f + H_LAG + 1, LAST) == e:
-                    quantise_h(f)
+            if e > H_LAG:
+                quantise_h(e - H_LAG - 1)
             quantise_w1(e)
+            if e == LAST:
+                quantise_h(e - H_LAG)
             if e < 2:
                 gather_words(2 * e)
                 gather_words(2 * e + 1)
@@ -326,22 +327,27 @@ def tile_moe_ogt_gelu_silu_kernel(
             nc.scalar.activation(o_tile[:], o_ps[:], ACT.Silu)
             return o_tile
 
-        parts, plain, total = ({} for i in range(3))
+        parts, plain, weighed, total = ({} for i in range(4))
 
         def entries(r, c):
             return pos_sb[r][:, c * CHUNK // 16 : (c + 1) * CHUNK // 16]
 
-        def fetch(r, c):
-            plain[r, c] = keep.tile([P, CHUNK], F32, name="plain%d_%d" % (r, c))
-            nc.scalar.activation(plain[r, c][:], y_sb[:].indirect(entries(r, c)), ACT.Copy)
+        def fetch(c):
+            plain[c] = keep.tile([P, 2, CHUNK], F32, name="plain%d" % c)
+            for r in range(2):
+                nc.scalar.activation(plain[c][:, r, :], y_sb[:].indirect(entries(r, c)), ACT.Copy)
 
         def fetch_weighted(r, c):
             parts[r, c] = keep.tile([P, CHUNK], F32, name="part%d_%d" % (r, c))
             nc.vector.tensor_tensor(parts[r, c][:], y_sb[:].indirect(entries(r, c)), gate_sb[c][:, r, :], ALU.mult)
 
-        def weigh(r, c):
-            parts[r, c] = keep.tile([P, CHUNK], F32, name="part%d_%d" % (r, c))
-            nc.vector.tensor_tensor(parts[r, c][:], plain[r, c][:], gate_sb[c][:, r, :], ALU.mult)
+        def weigh(c, lists):
+            if lists.start == 0:
+                both = keep.tile([P, 2, CHUNK], F32, name="parts%d" % c)
+                weighed[c] = both
+                for r in range(2):
+                    parts[r, c] = both[:, r, :]
+            nc.vector.tensor_tensor(weighed[c][:, lists, :], plain[c][:, lists, :], gate_sb[c][:, lists, :], ALU.mult)
 
         def add_turned(c):
             total[c] = bank([P, CHUNK], "turned", 6 + c)
@@ -378,9 +384,10 @@ def tile_moe_ogt_gelu_silu_kernel(
         def finish(c, o_tile):
             result = keep.tile([P, CHUNK], F32, name="result%d" % c)
             o_chunk = o_tile[:, (c - TURNED) * CHUNK : (c - TURNED + 1) * CHUNK]
-            for cols in pieces(c):
+            for i, cols in enumerate(pieces(c)):
                 nc.vector.tensor_tensor(result[:, cols], total[c][:, cols], o_chunk[:, cols], ALU.mult)
-            nc.sync.dma_start(out[:, c * CHUNK : (c + 1) * CHUNK], result[:])
+                queue = nc.sync if i == 0 else nc.scalar
+                queue.dma_start(out[:, c * CHUNK : (c + 1) * CHUNK][:, cols], result[:, cols])
 
         o_turned = output_gate_turned()
         for c in range(TURNED):
@@ -388,15 +395,13 @@ def tile_moe_ogt_gelu_silu_kernel(
             fetch_weighted(1, c)
             add_turned(c)
         for c in range(TURNED, T // CHUNK):
-            fetch(0, c)
-            fetch(1, c)
+            fetch(c)
         o_plain = output_gate_plain()
         backs = [finish_turned(c, o_turned) for c in range(TURNED)]
-        weigh(0, 2)
-        weigh(1, 2)
-        weigh(0, 3)
+        weigh(2, slice(0, 2))
+        weigh(3, slice(0, 1))
         add(2)
-        weigh(1, 3)
+        weigh(3, slice(1, 2))
         finish(2, o_plain)
         add(3)
         for c in range(TURNED):

@@ -89,13 +89,13 @@ def tile_moe_ogt_gelu_silu_kernel(
         def behind_rounding(e, at, shape, dtype, name):
             return reuse.tile(shape, dtype, name=name, align_bytes=64, offset=e * RAW + at)
 
+        nc.sync.dma_start(offs_sb[:], offs)
         for q in range(4):
             queue = nc.sync if q < 2 else nc.scalar
             queue.dma_start(
                 x_s[:].bitcast(I32)[32 * q : 32 * q + 32, :],
                 x_scales[0].bitcast(I32)[4 * q : 4 * q + 4, :].partition_broadcast(8),
             )
-        nc.sync.dma_start(offs_sb[:], offs)
         nc.scalar.activation(warm_out[:], warm[:], ACT.Gelu_apprx_tanh)
 
         def load_w2(a):
@@ -370,7 +370,7 @@ def tile_moe_ogt_gelu_silu_kernel(
         def store_turned(c, back):
             result = keep.tile([P, CHUNK], F32, name="result%d" % c)
             nc.scalar.copy(result[:], back[:])
-            nc.scalar.dma_start(out[:, c * CHUNK : (c + 1) * CHUNK], result[:])
+            nc.sync.dma_start(out[:, c * CHUNK : (c + 1) * CHUNK], result[:])
 
         def pieces(c):
             width = CHUNK if (c + 1) * CHUNK < T else P
@@ -384,10 +384,9 @@ def tile_moe_ogt_gelu_silu_kernel(
         def finish(c, o_tile):
             result = keep.tile([P, CHUNK], F32, name="result%d" % c)
             o_chunk = o_tile[:, (c - TURNED) * CHUNK : (c - TURNED + 1) * CHUNK]
-            for i, cols in enumerate(pieces(c)):
+            for cols in pieces(c):
                 nc.vector.tensor_tensor(result[:, cols], total[c][:, cols], o_chunk[:, cols], ALU.mult)
-                queue = nc.sync if i == 0 else nc.scalar
-                queue.dma_start(out[:, c * CHUNK : (c + 1) * CHUNK][:, cols], result[:, cols])
+            nc.sync.dma_start(out[:, c * CHUNK : (c + 1) * CHUNK], result[:])
 
         o_turned = output_gate_turned()
         for c in range(TURNED):

@@ -341,13 +341,13 @@ def tile_moe_ogt_gelu_silu_kernel(
             parts[r, c] = keep.tile([P, CHUNK], F32, name="part%d_%d" % (r, c))
             nc.vector.tensor_tensor(parts[r, c][:], y_sb[:].indirect(entries(r, c)), gate_sb[c][:, r, :], ALU.mult)
 
-        def weigh(c, lists):
+        def weigh(c, lists, engine):
             if lists.start == 0:
                 both = keep.tile([P, 2, CHUNK], F32, name="parts%d" % c)
                 weighed[c] = both
                 for r in range(2):
                     parts[r, c] = both[:, r, :]
-            nc.vector.tensor_tensor(weighed[c][:, lists, :], plain[c][:, lists, :], gate_sb[c][:, lists, :], ALU.mult)
+            engine.tensor_tensor(weighed[c][:, lists, :], plain[c][:, lists, :], gate_sb[c][:, lists, :], ALU.mult)
 
         def add_turned(c):
             total[c] = bank([P, CHUNK], "turned", 6 + c)
@@ -397,10 +397,11 @@ def tile_moe_ogt_gelu_silu_kernel(
             fetch(c)
         o_plain = output_gate_plain()
         backs = [finish_turned(c, o_turned) for c in range(TURNED)]
-        weigh(2, slice(0, 2))
-        weigh(3, slice(0, 1))
+        weigh(2, slice(0, 1), nc.gpsimd)
+        weigh(2, slice(1, 2), nc.vector)
+        weigh(3, slice(0, 1), nc.vector)
         add(2)
-        weigh(3, slice(1, 2))
+        weigh(3, slice(1, 2), nc.vector)
         finish(2, o_plain)
         add(3)
         for c in range(TURNED):

@@ -144,8 +144,8 @@ def tile_moe_ogt_gelu_silu_kernel(
                 w1_bf[e] = reuse.tile([P, PACK * H], BF16, name="w1_bf%d" % e, align_bytes=64, offset=AT_ROUNDED)
             else:
                 w1_bf[e] = keep.tile([P, PACK * H], BF16, name="w1_bf%d" % e, align_bytes=64)
-            dst = w1_bf[e][:].rearrange("p (t m j) -> p m j t", t=PACK, j=PACK)
-            src = w1_raw[e][:].rearrange("p j (m t) -> p m j t", t=PACK)
+            dst = w1_bf[e][:].rearrange("p (t m h g) -> p m h t g", t=PACK, h=2, g=2)
+            src = w1_raw[e][:].rearrange("p (h g) (m t) -> p m h t g", t=PACK, g=2)
             if scalar_alone(e):
                 nc.scalar.copy(dst, src)
             elif e == POOLED:

@@ -202,8 +202,8 @@ def tile_moe_ogt_gelu_silu_kernel(
                         stop=True,
                     )
                 nc.scalar.activation(
-                    h_bf[e][:, u * PACK * P : (u + 1) * PACK * P].rearrange("p (n t) -> p n t", t=PACK),
-                    h_ps[:].rearrange("p t n -> p n t"),
+                    h_bf[e][:, u * PACK * P : (u + 1) * PACK * P].rearrange("p (n g t) -> p n t g", t=PACK, g=2),
+                    h_ps[:].rearrange("p t (n g) -> p n t g", g=2),
                     ACT.Gelu_apprx_tanh,
                 )
 

from contextlib import ExitStack

import concourse.mybir as mybir
from concourse.masks import make_identity

K, T, E, C, H, N = 512, 1024, 8, 256, 512, 128
SLOTS = E * C
FLOPS = 2 * (K * N * T + SLOTS * K * H + SLOTS * H * N)

F32 = mybir.dt.float32
BF16 = mybir.dt.bfloat16
I32 = mybir.dt.int32
U32 = mybir.dt.uint32
U16 = mybir.dt.uint16
U8 = mybir.dt.uint8
FP8X4 = mybir.dt.float8_e4m3fn_x4
FP4X4 = mybir.dt.float4_e2m1fn_x4
ACT = mybir.ActivationFunctionType
ALU = mybir.AluOpType

P = 128
PACK = 4
PAIR = 2 * C
LAST = E - 1
BANK = 512

GATHER_PHASE = 4
POOLED = 2
WORDS_AFTER = 2
FIRST_W2_BEFORE = 6
H_LAG = 2
TURNED = 2
CHUNK = 256

RAW = PACK * H * 4
AT_H_BF = 0
AT_WORDS = RAW // 2
AT_H_Q = RAW // 2
AT_CODES = 3 * RAW // 4
AT_ROUNDED = E * RAW


def scalar_alone(e):
    return e < GATHER_PHASE and e != POOLED


def halved(e):
    return e >= GATHER_PHASE and e % 2 == 1


def gelu_waits_for(e):
    if 0 < e < GATHER_PHASE - 1:
        return GATHER_PHASE - 1
    return LAST if e == LAST - 1 else None


def tile_moe_ogt_gelu_silu_kernel(
    tc, x_words, x_scales, wg_words, wg_scales, w1, w2, gate, offs, pos1, pos2, out
):
    nc = tc.nc
    with ExitStack() as ctx:
        keep = ctx.enter_context(tc.tile_pool(name="keep", bufs=1))
        reuse = ctx.enter_context(tc.tile_pool(name="reuse", bufs=1))
        psum = ctx.enter_context(tc.psum_pool(name="psum", bufs=1))

        offs_sb = keep.tile([P, SLOTS // 16], U16, name="offs_sb")
        pos_sb = [keep.tile([P, T // 16], U16, name="pos%d_sb" % r) for r in range(2)]
        x_w = keep.tile([P, T], I32, name="x_w", align_bytes=64)
        x_s = keep.tile([P, T], U8, name="x_s", align_bytes=64)
        wg_w = keep.tile([P, 2 * N], U8, name="wg_w", align_bytes=64)
        wg_s = keep.tile([P, N], U8, name="wg_s", align_bytes=64)
        w1_raw = [
            reuse.tile([P, PACK, H], F32, name="w1_raw%d" % e, align_bytes=64, offset=e * RAW) for e in range(E)
        ]
        w2_raw = [keep.tile([P, 2, PACK, N], F32, name="w2_raw%d" % a, align_bytes=64) for a in range(E // 2)]
        gate_sb = [keep.tile([P, 2, CHUNK], F32, name="gate%d" % c) for c in range(T // CHUNK)]
        ident = keep.tile([P, P], F32, name="ident")
        make_identity(nc, ident[:])
        y_sb = keep.tile([P, SLOTS], F32, name="y_sb")
        warm = keep.tile([P, 8], F32, name="warm")
        warm_out = keep.tile([P, 8], F32, name="warm_out")

        nc.vector.memset(wg_s[:].bitcast(I32), 0)
        nc.vector.memset(warm[:], 0.0)

        def bank(shape, name, number):
            return psum.tile(shape, F32, name=name, tag="bank%d" % number)

        def behind_rounding(e, at, shape, dtype, name):
            return reuse.tile(shape, dtype, name=name, align_bytes=64, offset=e * RAW + at)

        nc.sync.dma_start(offs_sb[:], offs)
        for q in range(4):
            queue = nc.sync if q < 2 else nc.scalar
            queue.dma_start(
                x_s[:].bitcast(I32)[32 * q : 32 * q + 32, :],
                x_scales[0].bitcast(I32)[4 * q : 4 * q + 4, :].partition_broadcast(8),
            )
        nc.scalar.activation(warm_out[:], warm[:], ACT.Gelu_apprx_tanh)

        def load_w2(a):
            nc.sync.dma_start(
                w2_raw[a][:].rearrange("p e j n -> p e (j n)"),
                w2[2 * a : 2 * a + 2].rearrange("e (p j) n -> p e (j n)", j=PACK),
            )

        for e in range(E):
            if e == WORDS_AFTER:
                nc.sync.dma_start(x_w[:], x_words[0].rearrange("p t d -> p (t d)").bitcast(I32))
            if e == FIRST_W2_BEFORE:
                load_w2(0)
            nc.sync.dma_start(w1_raw[e][:], w1[e].rearrange("(p j) c -> p j c", j=PACK))
        for a in range(1, E // 2):
            load_w2(a)
        nc.sync.dma_start(wg_w[:].bitcast(I32), wg_words[0].bitcast(I32))
        for r in range(4):
            nc.sync.dma_start(wg_s[:].bitcast(I32)[r:P:32, :], wg_scales[0].bitcast(I32)[r:16:4, :])
        nc.sync.dma_start(pos_sb[0][:], pos1)
        nc.sync.dma_start(pos_sb[1][:], pos2)
        for c in range(T // CHUNK):
            nc.sync.dma_start(gate_sb[c][:], gate[:, :, c * CHUNK : (c + 1) * CHUNK].rearrange("r p t -> p r t"))

        w1_bf, w1_q, w1_s, xg_w, xg_s, h_bf, h_q, h_s, w2_bf, w2_q, w2_s = ({} for i in range(11))

        def gather_scales(a):
            xg_s[a] = keep.tile([P, PAIR], U8, name="xg_s%d" % a, align_bytes=64)
            nc.vector.tensor_copy(xg_s[a][:], x_s[:].indirect(offs_sb[:, a * PAIR // 16 : (a + 1) * PAIR // 16]))

        def gather_words(a):
            if a < POOLED:
                xg_w[a] = keep.tile([P, PAIR], U32, name="xg_w%d" % a, align_bytes=64)
            else:
                xg_w[a] = behind_rounding(POOLED - 1, AT_WORDS + a % 2 * 4 * PAIR, [P, PAIR], U32, "xg_w%d" % a)
            entries = offs_sb[:, a * PAIR // 16 : (a + 1) * PAIR // 16]
            width = C if a == 0 else PAIR
            for first in range(0, PAIR, width):
                nc.vector.tensor_copy(
                    xg_w[a][:, first : first + width],
                    x_w[:].bitcast(U32).indirect(entries[:, first // 16 : (first + width) // 16]),
                )

        def round_w1(e):
            if e in (POOLED - 1, POOLED):
                w1_bf[e] = reuse.tile([P, PACK * H], BF16, name="w1_bf%d" % e, align_bytes=64, offset=AT_ROUNDED)
            else:
                w1_bf[e] = keep.tile([P, PACK * H], BF16, name="w1_bf%d" % e, align_bytes=64)
            dst = w1_bf[e][:].rearrange("p (t m h g) -> p m h t g", t=PACK, h=2, g=2)
            src = w1_raw[e][:].rearrange("p (h g) (m t) -> p m h t g", t=PACK, g=2)
            if scalar_alone(e):
                nc.scalar.copy(dst, src)
            elif e == POOLED:
                nc.scalar.copy(dst[:, P // 2 :], src[:, P // 2 :])
                nc.gpsimd.tensor_scalar(
                    w1_bf[e][:].rearrange("p (t m j) -> p m t j", t=PACK, j=PACK)[:, : P // 2],
                    w1_raw[e][:].rearrange("p j (m t) -> p m t j", t=PACK)[:, : P // 2],
                    1.0,
                    0.0,
                    ALU.mult,
                    ALU.add,
                )
            elif halved(e):
                nc.vector.tensor_copy(dst[:, : P // 2], src[:, : P // 2])
                nc.scalar.copy(dst[:, P // 2 :], src[:, P // 2 :])
            else:
                nc.vector.tensor_copy(dst[:, :, :, 0:2], src[:, :, :, 0:2])
                nc.vector.tensor_copy(dst[:, :, :, 2:4], src[:, :, :, 2:4])

        def quantise_w1(e):
            if e == GATHER_PHASE - 1:
                w1_q[e] = behind_rounding(e + 1, AT_CODES, [P, H], U32, "w1_q%d" % e)
            else:
                w1_q[e] = keep.tile([P, H], U32, name="w1_q%d" % e, align_bytes=64)
            w1_s[e] = keep.tile([P, H], U8, name="w1_s%d" % e, align_bytes=64)
            width = H if e < GATHER_PHASE or (halved(e) and e < LAST) else H // 2
            for first in range(0, H, width):
                cols = slice(first, first + width)
                nc.vector.quantize_mx(
                    out=w1_q[e][:, cols].bitcast(FP8X4),
                    scales=w1_s[e][:, cols],
                    in_=w1_bf[e][:, PACK * first : PACK * (first + width)],
                )

        def first_layer(e):
            if gelu_waits_for(e) is not None:
                at = AT_H_BF + e % 2 * 2 * PACK * C
                h_bf[e] = behind_rounding(gelu_waits_for(e), at, [P, PACK * C], BF16, "h_bf%d" % e)
            else:
                h_bf[e] = keep.tile([P, PACK * C], BF16, name="h_bf%d" % e, align_bytes=64)
            a, first = divmod(e * C, PAIR)
            for u in range(C // P):
                slots = slice(first + u * P, first + (u + 1) * P)
                h_ps = bank([P, PACK, P], "h_ps", (2 * e + u) % 4)
                for t in range(PACK):
                    cols = slice(t * P, (t + 1) * P)
                    nc.tensor.matmul_mx(
                        out=h_ps[:, t, :],
                        lhsT=w1_q[e][:, cols].bitcast(FP8X4),
                        lhsT_scale=w1_s[e][:, cols],
                        rhs=xg_w[a][:, slots].bitcast(FP8X4),
                        rhs_scale=xg_s[a][:, slots],
                        start=True,
                        stop=True,
                    )
                nc.scalar.activation(
                    h_bf[e][:, u * PACK * P : (u + 1) * PACK * P].rearrange("p (n g t) -> p n t g", t=PACK, g=2),
                    h_ps[:].rearrange("p t (n g) -> p n t g", g=2),
                    ACT.Gelu_apprx_tanh,
                )

        def quantise_h(e):
            if e + H_LAG < E:
                h_q[e] = behind_rounding(e + H_LAG, AT_H_Q, [P, C], U32, "h_q%d" % e)
            else:
                h_q[e] = keep.tile([P, C], U32, name="h_q%d" % e, align_bytes=64)
            h_s[e] = keep.tile([P, C], U8, name="h_s%d" % e, align_bytes=64)
            width = P if e == LAST else C
            for first in range(0, C, width):
                cols = slice(first, first + width)
                nc.vector.quantize_mx(
                    out=h_q[e][:, cols].bitcast(FP8X4),
                    scales=h_s[e][:, cols],
                    in_=h_bf[e][:, PACK * first : PACK * (first + width)],
                )

        def round_w2(a):
            w2_bf[a] = keep.tile([P, 2 * PACK * N], BF16, name="w2_bf%d" % a, align_bytes=64)
            dst = w2_bf[a][:].rearrange("p (e c i j) -> p e c j i", e=2, i=PACK, j=PACK)
            src = w2_raw[a][:].rearrange("p e j (c i) -> p e c j i", i=PACK)
            for b in range(2):
                if b == 1 and a == 1:
                    nc.scalar.copy(dst[:, b], src[:, b])
                else:
                    nc.vector.tensor_copy(dst[:, b], src[:, b])

        def quantise_w2(a):
            w2_q[a] = keep.tile([P, 2 * N], U32, name="w2_q%d" % a, align_bytes=64)
            w2_s[a] = keep.tile([P, 2 * N], U8, name="w2_s%d" % a, align_bytes=64)
            for first in range(0, 2 * N, N):
                cols = slice(first, first + N)
                nc.vector.quantize_mx(
                    out=w2_q[a][:, cols].bitcast(FP8X4),
                    scales=w2_s[a][:, cols],
                    in_=w2_bf[a][:, PACK * first : PACK * (first + N)],
                )

        def second_product(y_ps, e, first, width):
            a, b = divmod(e, 2)
            nc.tensor.matmul_mx(
                out=y_ps,
                lhsT=w2_q[a][:, b * N : (b + 1) * N].bitcast(FP8X4),
                lhsT_scale=w2_s[a][:, b * N : (b + 1) * N],
                rhs=h_q[e][:, first : first + width].bitcast(FP8X4),
                rhs_scale=h_s[e][:, first : first + width],
                start=True,
                stop=True,
            )

        def second_layer(a):
            if a > 0:
                round_w2(a)
            quantise_w2(a)
            if 2 * a + 1 < LAST:
                y_ps = bank([P, PAIR], "y_ps", (4, 5, 0)[a])
                for b in range(2):
                    second_product(y_ps[:, b * C : (b + 1) * C], 2 * a + b, 0, C)
                nc.scalar.copy(y_sb[:, a * PAIR : (a + 1) * PAIR], y_ps[:])
            else:
                quantise_h(LAST - 1)
                quantise_h(LAST)
                for e, first, width, number in ((LAST - 1, 0, C, 1), (LAST, 0, P, 4), (LAST, P, P, 2)):
                    y_ps = bank([P, width], "y_ps", number)
                    second_product(y_ps[:], e, first, width)
                    slots = slice(e * C + first, e * C + first + width)
                    nc.vector.tensor_copy(y_sb[:, slots], y_ps[:])

        for a in range(E // 2):
            gather_scales(a)
        for e in range(E):
            round_w1(e)
            if e > H_LAG:
                quantise_h(e - H_LAG - 1)
            quantise_w1(e)
            if e == LAST:
                quantise_h(e - H_LAG)
            if e < 2:
                gather_words(2 * e)
                gather_words(2 * e + 1)
            if e == FIRST_W2_BEFORE - 1:
                round_w2(0)
            first_layer(e)
            if e == FIRST_W2_BEFORE - 1:
                second_layer(0)
        for a in range(1, E // 2):
            second_layer(a)

        half = TURNED * CHUNK

        def output_gate_turned():
            o_tile = keep.tile([P, half], F32, name="o_turned")
            o_ps = bank([P, half], "o_ps", 0)
            for b in range(half // P):
                block = slice(b * P, (b + 1) * P)
                nc.tensor.matmul_mx(
                    out=o_ps[:, block],
                    lhsT=x_w[:, block].bitcast(FP8X4),
                    lhsT_scale=x_s[:, block],
                    rhs=wg_w[:].bitcast(FP4X4),
                    rhs_scale=wg_s[:],
                    start=True,
                    stop=True,
                )
            nc.scalar.activation(o_tile[:], o_ps[:], ACT.Silu)
            return o_tile

        def output_gate_plain():
            o_tile = keep.tile([P, T - half], F32, name="o_plain")
            o_ps = bank([P, T - half], "o_ps", 2)
            nc.tensor.matmul_mx(
                out=o_ps[:],
                lhsT=wg_w[:].bitcast(FP4X4),
                lhsT_scale=wg_s[:],
                rhs=x_w[:, half:].bitcast(FP8X4),
                rhs_scale=x_s[:, half:],
                start=True,
                stop=True,
            )
            nc.scalar.activation(o_tile[:], o_ps[:], ACT.Silu)
            return o_tile

        parts, plain, weighed, total = ({} for i in range(4))

        def entries(r, c):
            return pos_sb[r][:, c * CHUNK // 16 : (c + 1) * CHUNK // 16]

        def fetch(c):
            plain[c] = keep.tile([P, 2, CHUNK], F32, name="plain%d" % c)
            for r in range(2):
                nc.scalar.activation(plain[c][:, r, :], y_sb[:].indirect(entries(r, c)), ACT.Copy)

        def fetch_weighted(r, c):
            parts[r, c] = keep.tile([P, CHUNK], F32, name="part%d_%d" % (r, c))
            nc.vector.tensor_tensor(parts[r, c][:], y_sb[:].indirect(entries(r, c)), gate_sb[c][:, r, :], ALU.mult)

        def weigh(c, lists, engine):
            if lists.start == 0:
                both = keep.tile([P, 2, CHUNK], F32, name="parts%d" % c)
                weighed[c] = both
                for r in range(2):
                    parts[r, c] = both[:, r, :]
            engine.tensor_tensor(weighed[c][:, lists, :], plain[c][:, lists, :], gate_sb[c][:, lists, :], ALU.mult)

        def add_turned(c):
            total[c] = bank([P, CHUNK], "turned", 6 + c)
            for b in range(CHUNK // P):
                cols = slice(b * P, (b + 1) * P)
                for r in range(2):
                    nc.tensor.matmul(
                        total[c][:, cols], parts[r, c][:, cols], ident[:], is_transpose=True, start=(r == 0), stop=(r == 1)
                    )

        def finish_turned(c, o_tile):
            scaled = keep.tile([P, CHUNK], F32, name="scaled%d" % c)
            nc.vector.tensor_tensor(scaled[:], total[c][:], o_tile[:, c * CHUNK : (c + 1) * CHUNK], ALU.mult)
            back = bank([P, CHUNK], "back", 3 + 2 * c)
            for b in range(CHUNK // P):
                cols = slice(b * P, (b + 1) * P)
                nc.tensor.transpose(back[:, cols], scaled[:, cols], ident[:])
            return back

        def store_turned(c, back):
            result = keep.tile([P, CHUNK], F32, name="result%d" % c)
            nc.scalar.copy(result[:], back[:])
            nc.sync.dma_start(out[:, c * CHUNK : (c + 1) * CHUNK], result[:])

        def pieces(c):
            width = CHUNK if (c + 1) * CHUNK < T else P
            return [slice(first, first + width) for first in range(0, CHUNK, width)]

        def add(c):
            total[c] = keep.tile([P, CHUNK], F32, name="both%d" % c)
            for cols in pieces(c):
                nc.vector.tensor_tensor(total[c][:, cols], parts[0, c][:, cols], parts[1, c][:, cols], ALU.add)

        def finish(c, o_tile):
            result = keep.tile([P, CHUNK], F32, name="result%d" % c)
            o_chunk = o_tile[:, (c - TURNED) * CHUNK : (c - TURNED + 1) * CHUNK]
            for cols in pieces(c):
                nc.vector.tensor_tensor(result[:, cols], total[c][:, cols], o_chunk[:, cols], ALU.mult)
            nc.sync.dma_start(out[:, c * CHUNK : (c + 1) * CHUNK], result[:])

        o_turned = output_gate_turned()
        for c in range(TURNED):
            fetch_weighted(0, c)
            fetch_weighted(1, c)
            add_turned(c)
        for c in range(TURNED, T // CHUNK):
            fetch(c)
        o_plain = output_gate_plain()
        backs = [finish_turned(c, o_turned) for c in range(TURNED)]
        weigh(2, slice(0, 1), nc.gpsimd)
        weigh(2, slice(1, 2), nc.vector)
        weigh(3, slice(0, 1), nc.vector)
        add(2)
        weigh(3, slice(1, 2), nc.vector)
        finish(2, o_plain)
        add(3)
        for c in range(TURNED):
            store_turned(c, backs[c])
        finish(3, o_plain)
